import numpy as np
import ml_dtypes


def mxq(x, axis, fmt="e4m3"):
    dtype, down = {"e4m3": (ml_dtypes.float8_e4m3fn, 7), "e5m2": (ml_dtypes.float8_e5m2, 14)}[fmt]
    v = np.moveaxis(np.asarray(x, np.float32).astype(ml_dtypes.bfloat16).astype(np.float64), axis, -1)
    blocks = v.reshape(v.shape[:-1] + (-1, 32))
    amax = np.abs(blocks).max(-1, keepdims=True)
    byte = np.maximum(np.where(amax > 0, np.frexp(amax)[1] - 1 + 127, 0) - down, 1)
    scale = np.exp2(byte - 127.0)
    codes = (blocks / scale).astype(np.float32).astype(dtype).astype(np.float64)
    return np.moveaxis((codes * scale).reshape(v.shape), -1, axis)


WIDE = False


def mx_kscale(k):
    if not WIDE:
        return np.ones(k)
    levels = np.array([10, -10, 5, -5, 0])
    if k % 512:
        return np.exp2(np.random.permutation(np.resize(levels, k // 32))).repeat(32)
    a = np.empty((k // 512, 16))
    for p in range(k // 512):
        a[p, :8] = np.random.permutation(np.resize(levels, 8))
        for g in range(8):
            far = levels[np.abs(levels - a[p, g]) >= 10]
            a[p, g + 8] = far[np.random.randint(len(far))]
    return np.exp2(a.ravel()).repeat(32)


def f64(x):
    return np.asarray(x).astype(np.float64)


def striped(idx):
    return np.tile(idx.reshape(-1, 16).T, (8, 1)).astype(np.uint16)


def unstriped(offs):
    return offs[:16].T.reshape(-1).astype(np.int64)


def pack_weight(w):
    k, n = w.shape
    w = f64(np.asarray(w, np.float32).astype(ml_dtypes.bfloat16)).reshape(k // 32, 32, n)
    amax = np.abs(w).max(1)
    byte = np.clip(np.where(amax > 0, np.frexp(amax)[1] - 1 + 127 - 7, 1), 1, 254)
    scaled = (w * np.exp2(127.0 - byte)[:, None, :]).reshape(k, n).astype(np.float32)
    words = np.ascontiguousarray(scaled.reshape(k // 512, 128, 4, n).transpose(0, 1, 3, 2)).astype(ml_dtypes.float8_e4m3fn).view(np.uint8)
    return words, np.ascontiguousarray(byte.astype(np.uint8).reshape(k // 512, 16, n))


def unpack_weight(words, scales):
    g, p, n, _ = words.shape
    vals = np.ascontiguousarray(words).view(ml_dtypes.float8_e4m3fn).astype(np.float64) * np.repeat(np.exp2(scales.astype(np.float64) - 127.0), 8, axis=1)[..., None]
    return vals.transpose(0, 1, 3, 2).reshape(g * 512, n)


def relu(v):
    return np.maximum(v, 0.0)


K, T, S, H, N, U = 512, 2048, 512, 512, 256, 1024


def setup_inputs():
    n = np.random.standard_normal
    s = mx_kscale(K)[:, None]
    u = mx_kscale(H)
    packed_xT = pack_weight(n((K, T)) * s)
    return {
        "x_words": packed_xT[0],
        "x_scales": packed_xT[1],
        "mem": (n((H, U)) * u[:, None]).astype(np.float32),
        "w1": (n((K, N)) / np.sqrt(2 * K) / s).astype(np.float32),
        "sr": (n((H, N)) / np.sqrt(2 * H) / u[:, None]).astype(np.float32),
        "thr": (-np.random.uniform(0.2, 0.8, (N, 1))).astype(np.float32),
        "offs": striped(np.random.permutation(T)[:S]),
        "slot": striped(np.random.permutation(U)[:S]),
    }


def reference(x_words, x_scales, mem, w1, sr, thr, offs, slot):
    h = f64(mem)[:, unstriped(slot)]
    xq = unpack_weight(x_words, x_scales)[:, unstriped(offs)]
    y = mxq(f64(sr), 0, "e4m3").T @ mxq(h, 0, "e4m3") + mxq(f64(w1), 0, "e4m3").T @ xq
    return relu(y + f64(thr))

@@ -1,0 +1,117 @@
+from contextlib import ExitStack
+
+import concourse.mybir as mybir
+
+K, T, S, H, N, U = 512, 2048, 512, 512, 256, 1024
+FLOPS = 2 * (K + H) * N * S
+
+F32 = mybir.dt.float32
+BF16 = mybir.dt.bfloat16
+I32 = mybir.dt.int32
+U32 = mybir.dt.uint32
+U16 = mybir.dt.uint16
+U8 = mybir.dt.uint8
+FP8X4 = mybir.dt.float8_e4m3fn_x4
+ACT = mybir.ActivationFunctionType
+ALU = mybir.AluOpType
+
+P = 128
+PACK = 4
+HALF = S // 2
+M_TILES = N // P
+
+
+def tile_picked_ylista_nn_p_kernel(tc, x_words, x_scales, mem, w1, sr, thr, offs, slot, out):
+    nc = tc.nc
+    with ExitStack() as ctx:
+        sb = ctx.enter_context(tc.tile_pool(name="sb", bufs=1))
+        psum = ctx.enter_context(tc.psum_pool(name="psum", bufs=1))
+
+        slot_t = sb.tile([P, S // 16], U16, name="slot_t")
+        offs_t = sb.tile([P, S // 16], U16, name="offs_t")
+        xs_win = sb.tile([P, T], U8, name="xs_win", align_bytes=64)
+        xs_got = sb.tile([P, S], U8, name="xs_got", align_bytes=64)
+        xs_plane = sb.tile([P, S], U8, name="xs_plane", align_bytes=64)
+        xw_win = sb.tile([P, T], I32, name="xw_win", align_bytes=64)
+        thr_t = sb.tile([P, M_TILES, 1], F32, name="thr_t")
+
+        nc.vector.memset(xs_win[0:P - 16, :].bitcast(I32), 0)
+        nc.vector.memset(xs_plane[:].bitcast(I32), 0)
+
+        nc.sync.dma_start(out=xs_win[P - 16:P, :].bitcast(I32), in_=x_scales[0].bitcast(I32))
+        nc.sync.dma_start(offs_t[:], offs)
+        nc.sync.dma_start(slot_t[:], slot)
+        mem_rows = mem.rearrange("(p t) u -> p t u", t=PACK)
+        mem_t = [sb.tile([P, U], F32, name=f"mem{t}", align_bytes=64) for t in range(PACK)]
+        for t in range(PACK):
+            nc.sync.dma_start(out=mem_t[t][:], in_=mem_rows[:, t, :])
+        sr_raw = sb.tile([P, PACK, N], F32, name="sr_raw", align_bytes=64)
+        w1_raw = sb.tile([P, PACK, N], F32, name="w1_raw", align_bytes=64)
+        nc.sync.dma_start(out=sr_raw[:], in_=sr.rearrange("(p t) m -> p t m", t=PACK))
+        nc.sync.dma_start(out=w1_raw[:], in_=w1.rearrange("(p t) m -> p t m", t=PACK))
+        nc.sync.dma_start(out=xw_win[:], in_=x_words[0].rearrange("p n t -> p (n t)").bitcast(I32))
+        with nc.allow_non_contiguous_dma(reason="one threshold a partition"):
+            nc.sync.dma_start(out=thr_t[:], in_=thr.rearrange("(c p) o -> p c o", p=P))
+
+        nc.vector.tensor_copy(xs_got[:], xs_win[:].indirect(offs_t[:]))
+        for q in range(4):
+            first = P - 16 + 4 * q
+            nc.sync.dma_start(out=xs_plane[32 * q:32 * q + 4, :].bitcast(I32), in_=xs_got[first:first + 4, :].bitcast(I32))
+
+        h_bf = sb.tile([P, S, PACK], BF16, name="h_bf", align_bytes=64)
+        pairs = [sb.tile([P, 2, S], BF16, name=f"pair{u}", align_bytes=64) for u in range(2)]
+        for t in range(PACK):
+            nc.vector.tensor_copy(pairs[t // 2][:, t % 2, :], mem_t[t][:].indirect(slot_t[:]))
+        nc.scalar.activation(h_bf[:, :, 0:2], pairs[0][:].rearrange("p t c -> p c t"), ACT.Copy)
+        nc.vector.tensor_copy(h_bf[:, :, 2:4], pairs[1][:].rearrange("p t c -> p c t"))
+
+        def weights(raw, name):
+            grouped = sb.tile([P, N, PACK], BF16, name=name + "_bf", align_bytes=64)
+            nc.scalar.activation(
+                grouped[:].rearrange("p (c i) t -> p c t i", i=4),
+                raw[:].rearrange("p t (c i) -> p c t i", i=4),
+                ACT.Copy,
+            )
+            return grouped
+
+        def quantise(grouped, width, name):
+            codes = sb.tile([P, width], U32, name=name + "_codes", align_bytes=64)
+            scales = sb.tile([P, width], U8, name=name + "_scales", align_bytes=64)
+            nc.vector.quantize_mx(out=codes[:].bitcast(FP8X4), scales=scales[:], in_=grouped[:].rearrange("p c t -> p (c t)"))
+            return codes, scales
+
+        sr_bf = weights(sr_raw, "sr")
+        w1_bf = weights(w1_raw, "w1")
+        sr_codes, sr_scales = quantise(sr_bf, N, "sr")
+        h_codes, h_scales = quantise(h_bf, S, "h")
+        w1_codes, w1_scales = quantise(w1_bf, N, "w1")
+
+        acc = [[psum.tile([P, HALF], F32, name=f"acc{a}{c}") for c in range(M_TILES)] for a in range(2)]
+        for c in range(M_TILES):
+            rows = slice(c * P, (c + 1) * P)
+            for a in range(2):
+                cols = slice(a * HALF, (a + 1) * HALF)
+                nc.tensor.matmul_mx(
+                    out=acc[a][c][:], lhsT=sr_codes[:, rows].bitcast(FP8X4), lhsT_scale=sr_scales[:, rows],
+                    rhs=h_codes[:, cols].bitcast(FP8X4), rhs_scale=h_scales[:, cols], start=True, stop=False)
+
+        out_v = out.rearrange("(c p) n -> p c n", p=P)
+        xw_got = [sb.tile([P, HALF], U32, name=f"xw_got{a}", align_bytes=64) for a in range(2)]
+        for a in range(2):
+            nc.vector.tensor_copy(xw_got[a][:], xw_win[:].bitcast(U32).indirect(offs_t[:, a * HALF // 16:(a + 1) * HALF // 16]))
+        for a in range(2):
+            cols = slice(a * HALF, (a + 1) * HALF)
+            res = sb.tile([P, M_TILES, HALF], F32, name=f"res{a}", align_bytes=64)
+            for c in range(M_TILES):
+                rows = slice(c * P, (c + 1) * P)
+                nc.tensor.matmul_mx(
+                    out=acc[a][c][:], lhsT=w1_codes[:, rows].bitcast(FP8X4), lhsT_scale=w1_scales[:, rows],
+                    rhs=xw_got[a][:].bitcast(FP8X4), rhs_scale=xs_plane[:, cols], start=False, stop=True)
+                if c == 1:
+                    nc.vector.tensor_scalar(res[:, c, :], acc[a][c][:], thr_t[:, c, :], 0.0, ALU.add, ALU.max)
+                else:
+                    nc.scalar.activation(res[:, c, :], acc[a][c][:], ACT.Relu, bias=thr_t[:, c, :])
+                if a == 1:
+                    (nc.sync if c == 1 else nc.scalar).dma_start(out=out_v[:, c, cols], in_=res[:, c, :])
+            if a == 0:
+                nc.sync.dma_start(out=out_v[:, :, cols], in_=res[:])

@@ -32,38 +32,45 @@ def tile_picked_ylista_nn_p_kernel(tc, x_words, x_scales, mem, w1, sr, thr, offs
         xs_win = sb.tile([P, T], U8, name="xs_win", align_bytes=64)
         xs_got = sb.tile([P, S], U8, name="xs_got", align_bytes=64)
         xs_plane = sb.tile([P, S], U8, name="xs_plane", align_bytes=64)
-        xw_win = sb.tile([P, T], I32, name="xw_win", align_bytes=64)
-        thr_t = sb.tile([P, M_TILES, 1], F32, name="thr_t")
 
         nc.vector.memset(xs_win[0:P - 16, :].bitcast(I32), 0)
         nc.vector.memset(xs_plane[:].bitcast(I32), 0)
 
-        nc.sync.dma_start(out=xs_win[P - 16:P, :].bitcast(I32), in_=x_scales[0].bitcast(I32))
+        nc.scalar.dma_start(out=xs_win[P - 16:P, :].bitcast(I32), in_=x_scales[0].bitcast(I32))
         nc.sync.dma_start(offs_t[:], offs)
-        nc.sync.dma_start(slot_t[:], slot)
         mem_rows = mem.rearrange("(p t) u -> p t u", t=PACK)
         mem_t = [sb.tile([P, U], F32, name=f"mem{t}", align_bytes=64) for t in range(PACK)]
         for t in range(PACK):
             nc.sync.dma_start(out=mem_t[t][:], in_=mem_rows[:, t, :])
+            if t == 0:
+                nc.sync.dma_start(slot_t[:], slot)
         sr_raw = sb.tile([P, PACK, N], F32, name="sr_raw", align_bytes=64)
         w1_raw = sb.tile([P, PACK, N], F32, name="w1_raw", align_bytes=64)
         nc.sync.dma_start(out=sr_raw[:], in_=sr.rearrange("(p t) m -> p t m", t=PACK))
         nc.sync.dma_start(out=w1_raw[:], in_=w1.rearrange("(p t) m -> p t m", t=PACK))
+        nc.vector.tensor_copy(xs_got[:], xs_win[:].indirect(offs_t[:]))
+        for q in range(4):
+            first = P - 16 + 4 * q
+            nc.gpsimd.dma_start(out=xs_plane[32 * q:32 * q + 4, :].bitcast(I32), in_=xs_got[first:first + 4, :].bitcast(I32))
+
+        xw_win = sb.tile([P, T], I32, name="xw_win", align_bytes=64)
+        thr_t = sb.tile([P, M_TILES, 1], F32, name="thr_t", align_bytes=64)
         nc.sync.dma_start(out=xw_win[:], in_=x_words[0].rearrange("p n t -> p (n t)").bitcast(I32))
         with nc.allow_non_contiguous_dma(reason="one threshold a partition"):
             nc.sync.dma_start(out=thr_t[:], in_=thr.rearrange("(c p) o -> p c o", p=P))
 
-        nc.vector.tensor_copy(xs_got[:], xs_win[:].indirect(offs_t[:]))
-        for q in range(4):
-            first = P - 16 + 4 * q
-            nc.sync.dma_start(out=xs_plane[32 * q:32 * q + 4, :].bitcast(I32), in_=xs_got[first:first + 4, :].bitcast(I32))
-
-        h_bf = sb.tile([P, S, PACK], BF16, name="h_bf", align_bytes=64)
+        h_bf = [sb.tile([P, HALF, PACK], BF16, name=f"h_bf{a}", align_bytes=64) for a in range(2)]
         pairs = [sb.tile([P, 2, S], BF16, name=f"pair{u}", align_bytes=64) for u in range(2)]
-        for t in range(PACK):
+        for t in range(PACK - 1):
             nc.vector.tensor_copy(pairs[t // 2][:, t % 2, :], mem_t[t][:].indirect(slot_t[:]))
-        nc.scalar.activation(h_bf[:, :, 0:2], pairs[0][:].rearrange("p t c -> p c t"), ACT.Copy)
-        nc.vector.tensor_copy(h_bf[:, :, 2:4], pairs[1][:].rearrange("p t c -> p c t"))
+        for a in range(2):
+            nc.vector.tensor_copy(pairs[1][:, 1, a * HALF:(a + 1) * HALF], mem_t[PACK - 1][:].indirect(slot_t[:, a * HALF // 16:(a + 1) * HALF // 16]))
+        for a in range(2):
+            cols = slice(a * HALF, (a + 1) * HALF)
+            nc.scalar.activation(h_bf[a][:, :, 0:2], pairs[0][:, :, cols].rearrange("p t c -> p c t"), ACT.Copy)
+        for a in range(2):
+            cols = slice(a * HALF, (a + 1) * HALF)
+            nc.vector.tensor_copy(h_bf[a][:, :, 2:4], pairs[1][:, :, cols].rearrange("p t c -> p c t"))
 
         def weights(raw, name):
             grouped = sb.tile([P, N, PACK], BF16, name=name + "_bf", align_bytes=64)
@@ -83,17 +90,16 @@ def tile_picked_ylista_nn_p_kernel(tc, x_words, x_scales, mem, w1, sr, thr, offs
         sr_bf = weights(sr_raw, "sr")
         w1_bf = weights(w1_raw, "w1")
         sr_codes, sr_scales = quantise(sr_bf, N, "sr")
-        h_codes, h_scales = quantise(h_bf, S, "h")
+        h_mx = [quantise(h_bf[a], HALF, f"h{a}") for a in range(2)]
         w1_codes, w1_scales = quantise(w1_bf, N, "w1")
 
         acc = [[psum.tile([P, HALF], F32, name=f"acc{a}{c}") for c in range(M_TILES)] for a in range(2)]
-        for c in range(M_TILES):
-            rows = slice(c * P, (c + 1) * P)
-            for a in range(2):
-                cols = slice(a * HALF, (a + 1) * HALF)
+        for a in range(2):
+            for c in range(M_TILES):
+                rows = slice(c * P, (c + 1) * P)
                 nc.tensor.matmul_mx(
                     out=acc[a][c][:], lhsT=sr_codes[:, rows].bitcast(FP8X4), lhsT_scale=sr_scales[:, rows],
-                    rhs=h_codes[:, cols].bitcast(FP8X4), rhs_scale=h_scales[:, cols], start=True, stop=False)
+                    rhs=h_mx[a][0][:].bitcast(FP8X4), rhs_scale=h_mx[a][1][:], start=True, stop=False)
 
         out_v = out.rearrange("(c p) n -> p c n", p=P)
         xw_got = [sb.tile([P, HALF], U32, name=f"xw_got{a}", align_bytes=64) for a in range(2)]
@@ -111,7 +117,4 @@ def tile_picked_ylista_nn_p_kernel(tc, x_words, x_scales, mem, w1, sr, thr, offs
                     nc.vector.tensor_scalar(res[:, c, :], acc[a][c][:], thr_t[:, c, :], 0.0, ALU.add, ALU.max)
                 else:
                     nc.scalar.activation(res[:, c, :], acc[a][c][:], ACT.Relu, bias=thr_t[:, c, :])
-                if a == 1:
-                    (nc.sync if c == 1 else nc.scalar).dma_start(out=out_v[:, c, cols], in_=res[:, c, :])
-            if a == 0:
-                nc.sync.dma_start(out=out_v[:, :, cols], in_=res[:])
+                (nc.sync if c == 1 else nc.scalar).dma_start(out=out_v[:, c, cols], in_=res[:, c, :])

@@ -72,13 +72,14 @@ def tile_picked_ylista_nn_p_kernel(tc, x_words, x_scales, mem, w1, sr, thr, offs
             cols = slice(a * HALF, (a + 1) * HALF)
             nc.vector.tensor_copy(h_bf[a][:, :, 2:4], pairs[1][:, :, cols].rearrange("p t c -> p c t"))
 
-        def weights(raw, name):
-            grouped = sb.tile([P, N, PACK], BF16, name=name + "_bf", align_bytes=64)
-            nc.scalar.activation(
-                grouped[:].rearrange("p (c i) t -> p c t i", i=4),
-                raw[:].rearrange("p t (c i) -> p c t i", i=4),
-                ACT.Copy,
-            )
+        def weights(raw, width, name, on_vector):
+            grouped = sb.tile([P, width, PACK], BF16, name=name + "_bf", align_bytes=64)
+            dst = grouped[:].rearrange("p (c i) t -> p c t i", i=4)
+            src = raw.rearrange("p t (c i) -> p c t i", i=4)
+            if on_vector:
+                nc.vector.tensor_copy(dst, src)
+            else:
+                nc.scalar.activation(dst, src, ACT.Copy)
             return grouped
 
         def quantise(grouped, width, name):
@@ -87,11 +88,11 @@ def tile_picked_ylista_nn_p_kernel(tc, x_words, x_scales, mem, w1, sr, thr, offs
             nc.vector.quantize_mx(out=codes[:].bitcast(FP8X4), scales=scales[:], in_=grouped[:].rearrange("p c t -> p (c t)"))
             return codes, scales
 
-        sr_bf = weights(sr_raw, "sr")
-        w1_bf = weights(w1_raw, "w1")
+        sr_bf = weights(sr_raw[:], N, "sr", False)
+        w1_bf = [weights(w1_raw[:, :, c * P:(c + 1) * P], P, f"w1{c}", c == 1) for c in range(M_TILES)]
         sr_codes, sr_scales = quantise(sr_bf, N, "sr")
         h_mx = [quantise(h_bf[a], HALF, f"h{a}") for a in range(2)]
-        w1_codes, w1_scales = quantise(w1_bf, N, "w1")
+        w1_mx = [quantise(w1_bf[c], P, f"w1{c}") for c in range(M_TILES)]
 
         acc = [[psum.tile([P, HALF], F32, name=f"acc{a}{c}") for c in range(M_TILES)] for a in range(2)]
         for a in range(2):
@@ -111,7 +112,7 @@ def tile_picked_ylista_nn_p_kernel(tc, x_words, x_scales, mem, w1, sr, thr, offs
             for c in range(M_TILES):
                 rows = slice(c * P, (c + 1) * P)
                 nc.tensor.matmul_mx(
-                    out=acc[a][c][:], lhsT=w1_codes[:, rows].bitcast(FP8X4), lhsT_scale=w1_scales[:, rows],
+                    out=acc[a][c][:], lhsT=w1_mx[c][0][:].bitcast(FP8X4), lhsT_scale=w1_mx[c][1][:],
                     rhs=xw_got[a][:].bitcast(FP8X4), rhs_scale=xs_plane[:, cols], start=False, stop=True)
                 if c == 1:
                     nc.vector.tensor_scalar(res[:, c, :], acc[a][c][:], thr_t[:, c, :], 0.0, ALU.add, ALU.max)

@@ -29,9 +29,9 @@ def tile_picked_ylista_nn_p_kernel(tc, x_words, x_scales, mem, w1, sr, thr, offs
 
         slot_t = sb.tile([P, S // 16], U16, name="slot_t")
         offs_t = sb.tile([P, S // 16], U16, name="offs_t")
-        xs_win = sb.tile([P, T], U8, name="xs_win", align_bytes=64)
-        xs_got = sb.tile([P, S], U8, name="xs_got", align_bytes=64)
-        xs_plane = sb.tile([P, S], U8, name="xs_plane", align_bytes=64)
+        xs_win = sb.tile([P, T], U8, name="xs_win", align_bytes=256)
+        xs_got = sb.tile([P, S], U8, name="xs_got", align_bytes=256)
+        xs_plane = sb.tile([P, S], U8, name="xs_plane", align_bytes=256)
 
         nc.vector.memset(xs_win[0:P - 16, :].bitcast(I32), 0)
         nc.vector.memset(xs_plane[:].bitcast(I32), 0)
@@ -39,13 +39,13 @@ def tile_picked_ylista_nn_p_kernel(tc, x_words, x_scales, mem, w1, sr, thr, offs
         nc.scalar.dma_start(out=xs_win[P - 16:P, :].bitcast(I32), in_=x_scales[0].bitcast(I32))
         nc.sync.dma_start(offs_t[:], offs)
         mem_rows = mem.rearrange("(p t) u -> p t u", t=PACK)
-        mem_t = [sb.tile([P, U], F32, name=f"mem{t}", align_bytes=64) for t in range(PACK)]
+        mem_t = [sb.tile([P, U], F32, name=f"mem{t}", align_bytes=256) for t in range(PACK)]
         for t in range(PACK):
             nc.sync.dma_start(out=mem_t[t][:], in_=mem_rows[:, t, :])
             if t == 0:
                 nc.sync.dma_start(slot_t[:], slot)
-        sr_raw = sb.tile([P, PACK, N], F32, name="sr_raw", align_bytes=64)
-        w1_raw = sb.tile([P, PACK, N], F32, name="w1_raw", align_bytes=64)
+        sr_raw = sb.tile([P, PACK, N], F32, name="sr_raw", align_bytes=256)
+        w1_raw = sb.tile([P, PACK, N], F32, name="w1_raw", align_bytes=256)
         nc.sync.dma_start(out=sr_raw[:], in_=sr.rearrange("(p t) m -> p t m", t=PACK))
         nc.sync.dma_start(out=w1_raw[:], in_=w1.rearrange("(p t) m -> p t m", t=PACK))
         nc.vector.tensor_copy(xs_got[:], xs_win[:].indirect(offs_t[:]))
@@ -53,14 +53,14 @@ def tile_picked_ylista_nn_p_kernel(tc, x_words, x_scales, mem, w1, sr, thr, offs
             first = P - 16 + 4 * q
             nc.gpsimd.dma_start(out=xs_plane[32 * q:32 * q + 4, :].bitcast(I32), in_=xs_got[first:first + 4, :].bitcast(I32))
 
-        xw_win = sb.tile([P, T], I32, name="xw_win", align_bytes=64)
-        thr_t = sb.tile([P, M_TILES, 1], F32, name="thr_t", align_bytes=64)
+        xw_win = sb.tile([P, T], I32, name="xw_win", align_bytes=256)
+        thr_t = sb.tile([P, M_TILES, 1], F32, name="thr_t", align_bytes=256)
         nc.sync.dma_start(out=xw_win[:], in_=x_words[0].rearrange("p n t -> p (n t)").bitcast(I32))
         with nc.allow_non_contiguous_dma(reason="one threshold a partition"):
             nc.sync.dma_start(out=thr_t[:], in_=thr.rearrange("(c p) o -> p c o", p=P))
 
-        h_bf = [sb.tile([P, HALF, PACK], BF16, name=f"h_bf{a}", align_bytes=64) for a in range(2)]
-        pairs = [sb.tile([P, 2, S], BF16, name=f"pair{u}", align_bytes=64) for u in range(2)]
+        h_bf = [sb.tile([P, HALF, PACK], BF16, name=f"h_bf{a}", align_bytes=256) for a in range(2)]
+        pairs = [sb.tile([P, 2, S], BF16, name=f"pair{u}", align_bytes=256) for u in range(2)]
         for t in range(PACK - 1):
             nc.vector.tensor_copy(pairs[t // 2][:, t % 2, :], mem_t[t][:].indirect(slot_t[:]))
         for a in range(2):
@@ -70,10 +70,11 @@ def tile_picked_ylista_nn_p_kernel(tc, x_words, x_scales, mem, w1, sr, thr, offs
             nc.scalar.activation(h_bf[a][:, :, 0:2], pairs[0][:, :, cols].rearrange("p t c -> p c t"), ACT.Copy)
         for a in range(2):
             cols = slice(a * HALF, (a + 1) * HALF)
-            nc.vector.tensor_copy(h_bf[a][:, :, 2:4], pairs[1][:, :, cols].rearrange("p t c -> p c t"))
+            src = pairs[1][:, :, cols].rearrange("p t c -> p c t")
+            nc.vector.tensor_copy(h_bf[a][:, :, 2:4], src)
 
         def weights(raw, width, name, on_vector):
-            grouped = sb.tile([P, width, PACK], BF16, name=name + "_bf", align_bytes=64)
+            grouped = sb.tile([P, width, PACK], BF16, name=name + "_bf", align_bytes=256)
             dst = grouped[:].rearrange("p (c i) t -> p c t i", i=4)
             src = raw.rearrange("p t (c i) -> p c t i", i=4)
             if on_vector:
@@ -83,39 +84,37 @@ def tile_picked_ylista_nn_p_kernel(tc, x_words, x_scales, mem, w1, sr, thr, offs
             return grouped
 
         def quantise(grouped, width, name):
-            codes = sb.tile([P, width], U32, name=name + "_codes", align_bytes=64)
-            scales = sb.tile([P, width], U8, name=name + "_scales", align_bytes=64)
+            codes = sb.tile([P, width], U32, name=name + "_codes", align_bytes=256)
+            scales = sb.tile([P, width], U8, name=name + "_scales", align_bytes=256)
             nc.vector.quantize_mx(out=codes[:].bitcast(FP8X4), scales=scales[:], in_=grouped[:].rearrange("p c t -> p (c t)"))
             return codes, scales
 
         sr_bf = weights(sr_raw[:], N, "sr", False)
-        w1_bf = [weights(w1_raw[:, :, c * P:(c + 1) * P], P, f"w1{c}", c == 1) for c in range(M_TILES)]
+        w1_bf = [weights(w1_raw[:, :, c * P:(c + 1) * P], P, f"w1{c}", False) for c in range(M_TILES)]
         sr_codes, sr_scales = quantise(sr_bf, N, "sr")
         h_mx = [quantise(h_bf[a], HALF, f"h{a}") for a in range(2)]
         w1_mx = [quantise(w1_bf[c], P, f"w1{c}") for c in range(M_TILES)]
 
-        acc = [[psum.tile([P, HALF], F32, name=f"acc{a}{c}") for c in range(M_TILES)] for a in range(2)]
-        for a in range(2):
-            for c in range(M_TILES):
-                rows = slice(c * P, (c + 1) * P)
-                nc.tensor.matmul_mx(
-                    out=acc[a][c][:], lhsT=sr_codes[:, rows].bitcast(FP8X4), lhsT_scale=sr_scales[:, rows],
-                    rhs=h_mx[a][0][:].bitcast(FP8X4), rhs_scale=h_mx[a][1][:], start=True, stop=False)
+        pieces = [(0, 0, 128), (0, 128, 128), (1, 0, HALF), (0, HALF, HALF), (1, HALF, HALF)]
+        acc = [psum.tile([P, n], F32, name=f"acc{i}") for i, (c, j0, n) in enumerate(pieces)]
+        for i, (c, j0, n) in enumerate(pieces):
+            rows = slice(c * P, (c + 1) * P)
+            a, cols = j0 // HALF, slice(j0 % HALF, j0 % HALF + n)
+            nc.tensor.matmul_mx(
+                out=acc[i][:], lhsT=sr_codes[:, rows].bitcast(FP8X4), lhsT_scale=sr_scales[:, rows],
+                rhs=h_mx[a][0][:, cols].bitcast(FP8X4), rhs_scale=h_mx[a][1][:, cols], start=True, stop=False)
 
-        out_v = out.rearrange("(c p) n -> p c n", p=P)
-        xw_got = [sb.tile([P, HALF], U32, name=f"xw_got{a}", align_bytes=64) for a in range(2)]
+        xw_got = [sb.tile([P, HALF], U32, name=f"xw_got{a}", align_bytes=256) for a in range(2)]
         for a in range(2):
             nc.vector.tensor_copy(xw_got[a][:], xw_win[:].bitcast(U32).indirect(offs_t[:, a * HALF // 16:(a + 1) * HALF // 16]))
-        for a in range(2):
-            cols = slice(a * HALF, (a + 1) * HALF)
-            res = sb.tile([P, M_TILES, HALF], F32, name=f"res{a}", align_bytes=64)
-            for c in range(M_TILES):
-                rows = slice(c * P, (c + 1) * P)
-                nc.tensor.matmul_mx(
-                    out=acc[a][c][:], lhsT=w1_mx[c][0][:].bitcast(FP8X4), lhsT_scale=w1_mx[c][1][:],
-                    rhs=xw_got[a][:].bitcast(FP8X4), rhs_scale=xs_plane[:, cols], start=False, stop=True)
-                if c == 1:
-                    nc.vector.tensor_scalar(res[:, c, :], acc[a][c][:], thr_t[:, c, :], 0.0, ALU.add, ALU.max)
-                else:
-                    nc.scalar.activation(res[:, c, :], acc[a][c][:], ACT.Relu, bias=thr_t[:, c, :])
-                (nc.sync if c == 1 else nc.scalar).dma_start(out=out_v[:, c, cols], in_=res[:, c, :])
+        for i, (c, j0, n) in enumerate(pieces):
+            a, cols = j0 // HALF, slice(j0 % HALF, j0 % HALF + n)
+            res = sb.tile([P, n], F32, name=f"res{i}", align_bytes=256)
+            nc.tensor.matmul_mx(
+                out=acc[i][:], lhsT=w1_mx[c][0][:].bitcast(FP8X4), lhsT_scale=w1_mx[c][1][:],
+                rhs=xw_got[a][:, cols].bitcast(FP8X4), rhs_scale=xs_plane[:, j0:j0 + n], start=False, stop=True)
+            if c == 1:
+                nc.vector.tensor_scalar(res[:], acc[i][:], thr_t[:, c, :], 0.0, ALU.add, ALU.max)
+            else:
+                nc.scalar.activation(res[:], acc[i][:], ACT.Relu, bias=thr_t[:, c, :])
+            nc.sync.dma_start(out=out[c * P:(c + 1) * P, j0:j0 + n], in_=res[:])

@@ -95,26 +95,30 @@ def tile_picked_ylista_nn_p_kernel(tc, x_words, x_scales, mem, w1, sr, thr, offs
         h_mx = [quantise(h_bf[a], HALF, f"h{a}") for a in range(2)]
         w1_mx = [quantise(w1_bf[c], P, f"w1{c}") for c in range(M_TILES)]
 
-        pieces = [(0, 0, 128), (0, 128, 128), (1, 0, HALF), (0, HALF, HALF), (1, HALF, HALF)]
-        acc = [psum.tile([P, n], F32, name=f"acc{i}") for i, (c, j0, n) in enumerate(pieces)]
-        for i, (c, j0, n) in enumerate(pieces):
-            rows = slice(c * P, (c + 1) * P)
-            a, cols = j0 // HALF, slice(j0 % HALF, j0 % HALF + n)
+        pieces = [(a, c, q) for a in range(2) for c in range(M_TILES) for q in range(2)]
+        acc = {piece: psum.tile([P, P], F32, name=f"acc{i}") for i, piece in enumerate(pieces)}
+        for a, c, q in pieces:
+            rows, cols = slice(c * P, (c + 1) * P), slice(q * P, (q + 1) * P)
             nc.tensor.matmul_mx(
-                out=acc[i][:], lhsT=sr_codes[:, rows].bitcast(FP8X4), lhsT_scale=sr_scales[:, rows],
+                out=acc[a, c, q][:], lhsT=sr_codes[:, rows].bitcast(FP8X4), lhsT_scale=sr_scales[:, rows],
                 rhs=h_mx[a][0][:, cols].bitcast(FP8X4), rhs_scale=h_mx[a][1][:, cols], start=True, stop=False)
 
         xw_got = [sb.tile([P, HALF], U32, name=f"xw_got{a}", align_bytes=256) for a in range(2)]
         for a in range(2):
             nc.vector.tensor_copy(xw_got[a][:], xw_win[:].bitcast(U32).indirect(offs_t[:, a * HALF // 16:(a + 1) * HALF // 16]))
-        for i, (c, j0, n) in enumerate(pieces):
-            a, cols = j0 // HALF, slice(j0 % HALF, j0 % HALF + n)
-            res = sb.tile([P, n], F32, name=f"res{i}", align_bytes=256)
+        res = {(a, c): sb.tile([P, HALF], F32, name=f"res{a}{c}", align_bytes=256) for a in range(2) for c in range(M_TILES)}
+        for a, c, q in pieces:
+            cols = slice(q * P, (q + 1) * P)
+            j0 = a * HALF + q * P
+            first = a == 0 and c == 0
             nc.tensor.matmul_mx(
-                out=acc[i][:], lhsT=w1_mx[c][0][:].bitcast(FP8X4), lhsT_scale=w1_mx[c][1][:],
-                rhs=xw_got[a][:, cols].bitcast(FP8X4), rhs_scale=xs_plane[:, j0:j0 + n], start=False, stop=True)
-            if c == 1:
-                nc.vector.tensor_scalar(res[:], acc[i][:], thr_t[:, c, :], 0.0, ALU.add, ALU.max)
+                out=acc[a, c, q][:], lhsT=w1_mx[c][0][:].bitcast(FP8X4), lhsT_scale=w1_mx[c][1][:],
+                rhs=xw_got[a][:, cols].bitcast(FP8X4), rhs_scale=xs_plane[:, j0:j0 + P], start=False, stop=True)
+            if q == 1 and not first:
+                nc.vector.tensor_scalar(res[a, c][:, cols], acc[a, c, q][:], thr_t[:, c, :], 0.0, ALU.add, ALU.max)
             else:
-                nc.scalar.activation(res[:], acc[i][:], ACT.Relu, bias=thr_t[:, c, :])
-            nc.sync.dma_start(out=out[c * P:(c + 1) * P, j0:j0 + n], in_=res[:])
+                nc.scalar.activation(res[a, c][:, cols], acc[a, c, q][:], ACT.Relu, bias=thr_t[:, c, :])
+            if first:
+                nc.sync.dma_start(out=out[c * P:(c + 1) * P, j0:j0 + P], in_=res[a, c][:, cols])
+            elif q == 1:
+                nc.sync.dma_start(out=out[c * P:(c + 1) * P, a * HALF:(a + 1) * HALF], in_=res[a, c][:])

@@ -1,6 +1,7 @@
 from contextlib import ExitStack
 
 import concourse.mybir as mybir
+from concourse.masks import make_identity
 
 K, T, S, H, N, U = 512, 2048, 512, 512, 256, 1024
 FLOPS = 2 * (K + H) * N * S
@@ -38,6 +39,15 @@ def tile_picked_ylista_nn_p_kernel(tc, x_words, x_scales, mem, w1, sr, thr, offs
 
         nc.scalar.dma_start(out=xs_win[P - 16:P, :].bitcast(I32), in_=x_scales[0].bitcast(I32))
         nc.sync.dma_start(offs_t[:], offs)
+        thr_rows = sb.tile([P, P], F32, name="thr_rows", align_bytes=256)
+        ident = sb.tile([P, P], F32, name="ident", align_bytes=256)
+        thr_t = sb.tile([P, M_TILES, 1], F32, name="thr_t", align_bytes=256)
+        nc.scalar.dma_start(out=thr_rows[P - M_TILES:P, :], in_=thr.rearrange("(c p) o -> c (p o)", p=P))
+        nc.gpsimd.memset(thr_rows[0:P - M_TILES, :], 0.0)
+        make_identity(nc, ident[:])
+        thr_ps = psum.tile([P, P], F32, name="acc7")
+        nc.tensor.transpose(thr_ps[:], thr_rows[:], ident[:])
+        nc.scalar.activation(thr_t[:, :, 0], thr_ps[:, P - M_TILES:P], ACT.Copy)
         mem_rows = mem.rearrange("(p t) u -> p t u", t=PACK)
         mem_t = [sb.tile([P, U], F32, name=f"mem{t}", align_bytes=256) for t in range(PACK)]
         for t in range(PACK):
@@ -54,10 +64,7 @@ def tile_picked_ylista_nn_p_kernel(tc, x_words, x_scales, mem, w1, sr, thr, offs
             nc.gpsimd.dma_start(out=xs_plane[32 * q:32 * q + 4, :].bitcast(I32), in_=xs_got[first:first + 4, :].bitcast(I32))
 
         xw_win = sb.tile([P, T], I32, name="xw_win", align_bytes=256)
-        thr_t = sb.tile([P, M_TILES, 1], F32, name="thr_t", align_bytes=256)
         nc.sync.dma_start(out=xw_win[:], in_=x_words[0].rearrange("p n t -> p (n t)").bitcast(I32))
-        with nc.allow_non_contiguous_dma(reason="one threshold a partition"):
-            nc.sync.dma_start(out=thr_t[:], in_=thr.rearrange("(c p) o -> p c o", p=P))
 
         h_bf = [sb.tile([P, HALF, PACK], BF16, name=f"h_bf{a}", align_bytes=256) for a in range(2)]
         pairs = [sb.tile([P, 2, S], BF16, name=f"pair{u}", align_bytes=256) for u in range(2)]

@@ -102,6 +102,11 @@ def tile_picked_ylista_nn_p_kernel(tc, x_words, x_scales, mem, w1, sr, thr, offs
         h_mx = [quantise(h_bf[a], HALF, f"h{a}") for a in range(2)]
         w1_mx = [quantise(w1_bf[c], P, f"w1{c}") for c in range(M_TILES)]
 
+        warm = psum.tile([P, HALF], F32, name="acc7")
+        nc.tensor.matmul_mx(
+            out=warm[:], lhsT=h_mx[0][0][:, 0:P].bitcast(FP8X4), lhsT_scale=h_mx[0][1][:, 0:P],
+            rhs=h_mx[0][0][:].bitcast(FP8X4), rhs_scale=h_mx[0][1][:], start=True, stop=True)
+
         pieces = [(a, c, q) for a in range(2) for c in range(M_TILES) for q in range(2)]
         acc = {piece: psum.tile([P, P], F32, name=f"acc{i}") for i, piece in enumerate(pieces)}
         for a, c, q in pieces:

@@ -55,9 +55,10 @@ def tile_picked_ylista_nn_p_kernel(tc, x_words, x_scales, mem, w1, sr, thr, offs
             if t == 0:
                 nc.sync.dma_start(slot_t[:], slot)
         sr_raw = sb.tile([P, PACK, N], F32, name="sr_raw", align_bytes=256)
-        w1_raw = sb.tile([P, PACK, N], F32, name="w1_raw", align_bytes=256)
+        w1_raw = [sb.tile([P, PACK, P], F32, name=f"w1_raw{c}", align_bytes=256) for c in range(M_TILES)]
+        w1_rows = w1.rearrange("(p t) m -> p t m", t=PACK)
         nc.sync.dma_start(out=sr_raw[:], in_=sr.rearrange("(p t) m -> p t m", t=PACK))
-        nc.sync.dma_start(out=w1_raw[:], in_=w1.rearrange("(p t) m -> p t m", t=PACK))
+        nc.sync.dma_start(out=w1_raw[0][:], in_=w1_rows[:, :, 0:P])
         nc.vector.tensor_copy(xs_got[:], xs_win[:].indirect(offs_t[:]))
         for q in range(4):
             first = P - 16 + 4 * q
@@ -65,6 +66,7 @@ def tile_picked_ylista_nn_p_kernel(tc, x_words, x_scales, mem, w1, sr, thr, offs
 
         xw_win = sb.tile([P, T], I32, name="xw_win", align_bytes=256)
         nc.sync.dma_start(out=xw_win[:], in_=x_words[0].rearrange("p n t -> p (n t)").bitcast(I32))
+        nc.sync.dma_start(out=w1_raw[1][:], in_=w1_rows[:, :, P:2 * P])
 
         h_bf = [sb.tile([P, HALF, PACK], BF16, name=f"h_bf{a}", align_bytes=256) for a in range(2)]
         pairs = [sb.tile([P, 2, S], BF16, name=f"pair{u}", align_bytes=256) for u in range(2)]
@@ -80,14 +82,11 @@ def tile_picked_ylista_nn_p_kernel(tc, x_words, x_scales, mem, w1, sr, thr, offs
             src = pairs[1][:, :, cols].rearrange("p t c -> p c t")
             nc.vector.tensor_copy(h_bf[a][:, :, 2:4], src)
 
-        def weights(raw, width, name, on_vector):
+        def weights(raw, width, name):
             grouped = sb.tile([P, width, PACK], BF16, name=name + "_bf", align_bytes=256)
             dst = grouped[:].rearrange("p (c i) t -> p c t i", i=4)
             src = raw.rearrange("p t (c i) -> p c t i", i=4)
-            if on_vector:
-                nc.vector.tensor_copy(dst, src)
-            else:
-                nc.scalar.activation(dst, src, ACT.Copy)
+            nc.scalar.activation(dst, src, ACT.Copy)
             return grouped
 
         def quantise(grouped, width, name):
@@ -96,41 +95,35 @@ def tile_picked_ylista_nn_p_kernel(tc, x_words, x_scales, mem, w1, sr, thr, offs
             nc.vector.quantize_mx(out=codes[:].bitcast(FP8X4), scales=scales[:], in_=grouped[:].rearrange("p c t -> p (c t)"))
             return codes, scales
 
-        sr_bf = weights(sr_raw[:], N, "sr", False)
-        w1_bf = [weights(w1_raw[:, :, c * P:(c + 1) * P], P, f"w1{c}", False) for c in range(M_TILES)]
+        sr_bf = weights(sr_raw[:], N, "sr")
+        w1_bf = [weights(w1_raw[c][:], P, f"w1{c}") for c in range(M_TILES)]
         sr_codes, sr_scales = quantise(sr_bf, N, "sr")
         h_mx = [quantise(h_bf[a], HALF, f"h{a}") for a in range(2)]
-        w1_mx = [quantise(w1_bf[c], P, f"w1{c}") for c in range(M_TILES)]
+        w1_mx = [quantise(w1_bf[0], P, "w10")]
 
-        warm = psum.tile([P, HALF], F32, name="acc7")
-        nc.tensor.matmul_mx(
-            out=warm[:], lhsT=h_mx[0][0][:, 0:P].bitcast(FP8X4), lhsT_scale=h_mx[0][1][:, 0:P],
-            rhs=h_mx[0][0][:].bitcast(FP8X4), rhs_scale=h_mx[0][1][:], start=True, stop=True)
-
-        pieces = [(a, c, q) for a in range(2) for c in range(M_TILES) for q in range(2)]
-        acc = {piece: psum.tile([P, P], F32, name=f"acc{i}") for i, piece in enumerate(pieces)}
-        for a, c, q in pieces:
-            rows, cols = slice(c * P, (c + 1) * P), slice(q * P, (q + 1) * P)
+        pieces = [(0, a * HALF, HALF) for a in range(2)] + [(1, j0, P) for j0 in range(0, S, P)]
+        acc = {piece: psum.tile([P, piece[2]], F32, name=f"acc{i}") for i, piece in enumerate(pieces)}
+        for c, j0, width in sorted(pieces, key=lambda piece: piece[1] // HALF):
+            rows, cols = slice(c * P, (c + 1) * P), slice(j0 % HALF, j0 % HALF + width)
+            codes, scales = h_mx[j0 // HALF]
             nc.tensor.matmul_mx(
-                out=acc[a, c, q][:], lhsT=sr_codes[:, rows].bitcast(FP8X4), lhsT_scale=sr_scales[:, rows],
-                rhs=h_mx[a][0][:, cols].bitcast(FP8X4), rhs_scale=h_mx[a][1][:, cols], start=True, stop=False)
+                out=acc[c, j0, width][:], lhsT=sr_codes[:, rows].bitcast(FP8X4), lhsT_scale=sr_scales[:, rows],
+                rhs=codes[:, cols].bitcast(FP8X4), rhs_scale=scales[:, cols], start=True, stop=False)
 
         xw_got = [sb.tile([P, HALF], U32, name=f"xw_got{a}", align_bytes=256) for a in range(2)]
         for a in range(2):
             nc.vector.tensor_copy(xw_got[a][:], xw_win[:].bitcast(U32).indirect(offs_t[:, a * HALF // 16:(a + 1) * HALF // 16]))
-        res = {(a, c): sb.tile([P, HALF], F32, name=f"res{a}{c}", align_bytes=256) for a in range(2) for c in range(M_TILES)}
-        for a, c, q in pieces:
-            cols = slice(q * P, (q + 1) * P)
-            j0 = a * HALF + q * P
-            first = a == 0 and c == 0
+        w1_mx.append(quantise(w1_bf[1], P, "w11"))
+        res = [sb.tile([P, S], F32, name=name, align_bytes=256) for name in ("w1_raw1", "res1")]
+        for c, j0, width in pieces:
+            cols = slice(j0 % HALF, j0 % HALF + width)
             nc.tensor.matmul_mx(
-                out=acc[a, c, q][:], lhsT=w1_mx[c][0][:].bitcast(FP8X4), lhsT_scale=w1_mx[c][1][:],
-                rhs=xw_got[a][:, cols].bitcast(FP8X4), rhs_scale=xs_plane[:, j0:j0 + P], start=False, stop=True)
-            if q == 1 and not first:
-                nc.vector.tensor_scalar(res[a, c][:, cols], acc[a, c, q][:], thr_t[:, c, :], 0.0, ALU.add, ALU.max)
+                out=acc[c, j0, width][:], lhsT=w1_mx[c][0][:].bitcast(FP8X4), lhsT_scale=w1_mx[c][1][:],
+                rhs=xw_got[j0 // HALF][:, cols].bitcast(FP8X4), rhs_scale=xs_plane[:, j0:j0 + width], start=False, stop=True)
+            if c == 1 and j0 != HALF:
+                nc.vector.tensor_scalar(res[c][:, j0:j0 + width], acc[c, j0, width][:], thr_t[:, c, :], 0.0, ALU.add, ALU.max)
             else:
-                nc.scalar.activation(res[a, c][:, cols], acc[a, c, q][:], ACT.Relu, bias=thr_t[:, c, :])
-            if first:
-                nc.sync.dma_start(out=out[c * P:(c + 1) * P, j0:j0 + P], in_=res[a, c][:, cols])
-            elif q == 1:
-                nc.sync.dma_start(out=out[c * P:(c + 1) * P, a * HALF:(a + 1) * HALF], in_=res[a, c][:])
+                nc.scalar.activation(res[c][:, j0:j0 + width], acc[c, j0, width][:], ACT.Relu, bias=thr_t[:, c, :])
+            if (j0 + width) % HALF == 0:
+                half = slice(j0 + width - HALF, j0 + width)
+                nc.sync.dma_start(out=out[c * P:(c + 1) * P, half], in_=res[c][:, half])

@@ -82,12 +82,8 @@ def tile_picked_ylista_nn_p_kernel(tc, x_words, x_scales, mem, w1, sr, thr, offs
             src = pairs[1][:, :, cols].rearrange("p t c -> p c t")
             nc.vector.tensor_copy(h_bf[a][:, :, 2:4], src)
 
-        def weights(raw, width, name):
-            grouped = sb.tile([P, width, PACK], BF16, name=name + "_bf", align_bytes=256)
-            dst = grouped[:].rearrange("p (c i) t -> p c t i", i=4)
-            src = raw.rearrange("p t (c i) -> p c t i", i=4)
-            nc.scalar.activation(dst, src, ACT.Copy)
-            return grouped
+        def interleave(grouped, raw, cols):
+            return grouped[:, cols, :].rearrange("p (c i) t -> p c t i", i=4), raw[:, :, cols].rearrange("p t (c i) -> p c t i", i=4)
 
         def quantise(grouped, width, name):
             codes = sb.tile([P, width], U32, name=name + "_codes", align_bytes=256)
@@ -95,8 +91,12 @@ def tile_picked_ylista_nn_p_kernel(tc, x_words, x_scales, mem, w1, sr, thr, offs
             nc.vector.quantize_mx(out=codes[:].bitcast(FP8X4), scales=scales[:], in_=grouped[:].rearrange("p c t -> p (c t)"))
             return codes, scales
 
-        sr_bf = weights(sr_raw[:], N, "sr")
-        w1_bf = [weights(w1_raw[c][:], P, f"w1{c}") for c in range(M_TILES)]
+        sr_bf = sb.tile([P, N, PACK], BF16, name="sr_bf", align_bytes=256)
+        w1_bf = [sb.tile([P, P, PACK], BF16, name=f"w1_bf{c}", align_bytes=256) for c in range(M_TILES)]
+        nc.scalar.activation(*interleave(sr_bf, sr_raw, slice(0, N)), ACT.Copy)
+        nc.scalar.activation(*interleave(w1_bf[0], w1_raw[0], slice(0, P)), ACT.Copy)
+        nc.scalar.activation(*interleave(w1_bf[1], w1_raw[1], slice(0, P // 2)), ACT.Copy)
+        nc.gpsimd.tensor_scalar(*interleave(w1_bf[1], w1_raw[1], slice(P // 2, P)), 1.0, 0.0, ALU.mult, ALU.add)
         sr_codes, sr_scales = quantise(sr_bf, N, "sr")
         h_mx = [quantise(h_bf[a], HALF, f"h{a}") for a in range(2)]
         w1_mx = [quantise(w1_bf[0], P, "w10")]
@@ -114,13 +114,13 @@ def tile_picked_ylista_nn_p_kernel(tc, x_words, x_scales, mem, w1, sr, thr, offs
         for a in range(2):
             nc.vector.tensor_copy(xw_got[a][:], xw_win[:].bitcast(U32).indirect(offs_t[:, a * HALF // 16:(a + 1) * HALF // 16]))
         w1_mx.append(quantise(w1_bf[1], P, "w11"))
-        res = [sb.tile([P, S], F32, name=name, align_bytes=256) for name in ("w1_raw1", "res1")]
+        res = [sb.tile([P, S], F32, name=f"res{c}", align_bytes=256) for c in range(M_TILES)]
         for c, j0, width in pieces:
             cols = slice(j0 % HALF, j0 % HALF + width)
             nc.tensor.matmul_mx(
                 out=acc[c, j0, width][:], lhsT=w1_mx[c][0][:].bitcast(FP8X4), lhsT_scale=w1_mx[c][1][:],
                 rhs=xw_got[j0 // HALF][:, cols].bitcast(FP8X4), rhs_scale=xs_plane[:, j0:j0 + width], start=False, stop=True)
-            if c == 1 and j0 != HALF:
+            if c == 1 and j0 % HALF == 0:
                 nc.vector.tensor_scalar(res[c][:, j0:j0 + width], acc[c, j0, width][:], thr_t[:, c, :], 0.0, ALU.add, ALU.max)
             else:
                 nc.scalar.activation(res[c][:, j0:j0 + width], acc[c, j0, width][:], ACT.Relu, bias=thr_t[:, c, :])

@@ -85,8 +85,8 @@ def tile_picked_ylista_nn_p_kernel(tc, x_words, x_scales, mem, w1, sr, thr, offs
         def interleave(grouped, raw, cols):
             return grouped[:, cols, :].rearrange("p (c i) t -> p c t i", i=4), raw[:, :, cols].rearrange("p t (c i) -> p c t i", i=4)
 
-        def quantise(grouped, width, name):
-            codes = sb.tile([P, width], U32, name=name + "_codes", align_bytes=256)
+        def quantise(grouped, width, name, codes_name):
+            codes = sb.tile([P, width], U32, name=codes_name, align_bytes=256)
             scales = sb.tile([P, width], U8, name=name + "_scales", align_bytes=256)
             nc.vector.quantize_mx(out=codes[:].bitcast(FP8X4), scales=scales[:], in_=grouped[:].rearrange("p c t -> p (c t)"))
             return codes, scales
@@ -97,9 +97,14 @@ def tile_picked_ylista_nn_p_kernel(tc, x_words, x_scales, mem, w1, sr, thr, offs
         nc.scalar.activation(*interleave(w1_bf[0], w1_raw[0], slice(0, P)), ACT.Copy)
         nc.scalar.activation(*interleave(w1_bf[1], w1_raw[1], slice(0, P // 2)), ACT.Copy)
         nc.gpsimd.tensor_scalar(*interleave(w1_bf[1], w1_raw[1], slice(P // 2, P)), 1.0, 0.0, ALU.mult, ALU.add)
-        sr_codes, sr_scales = quantise(sr_bf, N, "sr")
-        h_mx = [quantise(h_bf[a], HALF, f"h{a}") for a in range(2)]
-        w1_mx = [quantise(w1_bf[0], P, "w10")]
+        sr_codes, sr_scales = quantise(sr_bf, N, "sr", "sr_codes")
+        h_mx = [quantise(h_bf[a], HALF, f"h{a}", name) for a, name in enumerate(("h0_codes", "sr_bf"))]
+        w1_mx = [quantise(w1_bf[0], P, "w10", "w10_codes")]
+
+        warm = psum.tile([P, HALF], F32, name="acc6")
+        nc.tensor.matmul_mx(
+            out=warm[:], lhsT=h_mx[0][0][:, 0:P].bitcast(FP8X4), lhsT_scale=h_mx[0][1][:, 0:P],
+            rhs=h_mx[0][0][:].bitcast(FP8X4), rhs_scale=h_mx[0][1][:], start=True, stop=True)
 
         pieces = [(0, a * HALF, HALF) for a in range(2)] + [(1, j0, P) for j0 in range(0, S, P)]
         acc = {piece: psum.tile([P, piece[2]], F32, name=f"acc{i}") for i, piece in enumerate(pieces)}
@@ -113,7 +118,7 @@ def tile_picked_ylista_nn_p_kernel(tc, x_words, x_scales, mem, w1, sr, thr, offs
         xw_got = [sb.tile([P, HALF], U32, name=f"xw_got{a}", align_bytes=256) for a in range(2)]
         for a in range(2):
             nc.vector.tensor_copy(xw_got[a][:], xw_win[:].bitcast(U32).indirect(offs_t[:, a * HALF // 16:(a + 1) * HALF // 16]))
-        w1_mx.append(quantise(w1_bf[1], P, "w11"))
+        w1_mx.append(quantise(w1_bf[1], P, "w11", "w11_codes"))
         res = [sb.tile([P, S], F32, name=f"res{c}", align_bytes=256) for c in range(M_TILES)]
         for c, j0, width in pieces:
             cols = slice(j0 % HALF, j0 % HALF + width)

@@ -42,18 +42,18 @@ def tile_picked_ylista_nn_p_kernel(tc, x_words, x_scales, mem, w1, sr, thr, offs
         thr_rows = sb.tile([P, P], F32, name="thr_rows", align_bytes=256)
         ident = sb.tile([P, P], F32, name="ident", align_bytes=256)
         thr_t = sb.tile([P, M_TILES, 1], F32, name="thr_t", align_bytes=256)
-        nc.scalar.dma_start(out=thr_rows[P - M_TILES:P, :], in_=thr.rearrange("(c p) o -> c (p o)", p=P))
-        nc.gpsimd.memset(thr_rows[0:P - M_TILES, :], 0.0)
-        make_identity(nc, ident[:])
-        thr_ps = psum.tile([P, P], F32, name="acc7")
-        nc.tensor.transpose(thr_ps[:], thr_rows[:], ident[:])
-        nc.scalar.activation(thr_t[:, :, 0], thr_ps[:, P - M_TILES:P], ACT.Copy)
         mem_rows = mem.rearrange("(p t) u -> p t u", t=PACK)
         mem_t = [sb.tile([P, U], F32, name=f"mem{t}", align_bytes=256) for t in range(PACK)]
         for t in range(PACK):
             nc.sync.dma_start(out=mem_t[t][:], in_=mem_rows[:, t, :])
             if t == 0:
                 nc.sync.dma_start(slot_t[:], slot)
+        nc.sync.dma_start(out=thr_rows[P - M_TILES:P, :], in_=thr.rearrange("(c p) o -> c (p o)", p=P))
+        nc.gpsimd.memset(thr_rows[0:P - M_TILES, :], 0.0)
+        make_identity(nc, ident[:])
+        thr_ps = psum.tile([P, P], F32, name="acc7")
+        nc.tensor.transpose(thr_ps[:], thr_rows[:], ident[:])
+        nc.scalar.activation(thr_t[:, :, 0], thr_ps[:, P - M_TILES:P], ACT.Copy)
         sr_raw = sb.tile([P, PACK, N], F32, name="sr_raw", align_bytes=256)
         w1_raw = [sb.tile([P, PACK, P], F32, name=f"w1_raw{c}", align_bytes=256) for c in range(M_TILES)]
         w1_rows = w1.rearrange("(p t) m -> p t m", t=PACK)
@@ -91,44 +91,45 @@ def tile_picked_ylista_nn_p_kernel(tc, x_words, x_scales, mem, w1, sr, thr, offs
             nc.vector.quantize_mx(out=codes[:].bitcast(FP8X4), scales=scales[:], in_=grouped[:].rearrange("p c t -> p (c t)"))
             return codes, scales
 
-        sr_bf = sb.tile([P, N, PACK], BF16, name="sr_bf", align_bytes=256)
+        sr_bf = [sb.tile([P, P, PACK], BF16, name=f"sr_bf{c}", align_bytes=256) for c in range(M_TILES)]
         w1_bf = [sb.tile([P, P, PACK], BF16, name=f"w1_bf{c}", align_bytes=256) for c in range(M_TILES)]
-        nc.scalar.activation(*interleave(sr_bf, sr_raw, slice(0, N)), ACT.Copy)
+        for c in range(M_TILES):
+            nc.scalar.activation(*interleave(sr_bf[c], sr_raw[:, :, c * P:(c + 1) * P], slice(0, P)), ACT.Copy)
         nc.scalar.activation(*interleave(w1_bf[0], w1_raw[0], slice(0, P)), ACT.Copy)
-        nc.scalar.activation(*interleave(w1_bf[1], w1_raw[1], slice(0, P // 2)), ACT.Copy)
-        nc.gpsimd.tensor_scalar(*interleave(w1_bf[1], w1_raw[1], slice(P // 2, P)), 1.0, 0.0, ALU.mult, ALU.add)
-        sr_codes, sr_scales = quantise(sr_bf, N, "sr", "sr_codes")
-        h_mx = [quantise(h_bf[a], HALF, f"h{a}", name) for a, name in enumerate(("h0_codes", "sr_bf"))]
+        nc.scalar.activation(*interleave(w1_bf[1], w1_raw[1], slice(0, 3 * P // 4)), ACT.Copy)
+        nc.gpsimd.tensor_scalar(*interleave(w1_bf[1], w1_raw[1], slice(3 * P // 4, P)), 1.0, 0.0, ALU.mult, ALU.add)
+        sr_mx = [quantise(sr_bf[c], P, f"sr{c}", f"sr{c}_codes") for c in range(M_TILES)]
+        h_mx = [quantise(h_bf[a], HALF, f"h{a}", name) for a, name in enumerate(("h0_codes", "sr_bf1"))]
         w1_mx = [quantise(w1_bf[0], P, "w10", "w10_codes")]
 
-        warm = psum.tile([P, HALF], F32, name="acc6")
+        warm = psum.tile([P, HALF], F32, name="acc7")
         nc.tensor.matmul_mx(
             out=warm[:], lhsT=h_mx[0][0][:, 0:P].bitcast(FP8X4), lhsT_scale=h_mx[0][1][:, 0:P],
             rhs=h_mx[0][0][:].bitcast(FP8X4), rhs_scale=h_mx[0][1][:], start=True, stop=True)
 
-        pieces = [(0, a * HALF, HALF) for a in range(2)] + [(1, j0, P) for j0 in range(0, S, P)]
+        pieces = [(0, 0, HALF)] + [(0, j0, P) for j0 in range(HALF, S, P)] + [(1, j0, P) for j0 in range(0, S, P)]
         acc = {piece: psum.tile([P, piece[2]], F32, name=f"acc{i}") for i, piece in enumerate(pieces)}
         for c, j0, width in sorted(pieces, key=lambda piece: piece[1] // HALF):
-            rows, cols = slice(c * P, (c + 1) * P), slice(j0 % HALF, j0 % HALF + width)
+            cols = slice(j0 % HALF, j0 % HALF + width)
             codes, scales = h_mx[j0 // HALF]
             nc.tensor.matmul_mx(
-                out=acc[c, j0, width][:], lhsT=sr_codes[:, rows].bitcast(FP8X4), lhsT_scale=sr_scales[:, rows],
+                out=acc[c, j0, width][:], lhsT=sr_mx[c][0][:].bitcast(FP8X4), lhsT_scale=sr_mx[c][1][:],
                 rhs=codes[:, cols].bitcast(FP8X4), rhs_scale=scales[:, cols], start=True, stop=False)
 
         xw_got = [sb.tile([P, HALF], U32, name=f"xw_got{a}", align_bytes=256) for a in range(2)]
         for a in range(2):
             nc.vector.tensor_copy(xw_got[a][:], xw_win[:].bitcast(U32).indirect(offs_t[:, a * HALF // 16:(a + 1) * HALF // 16]))
         w1_mx.append(quantise(w1_bf[1], P, "w11", "w11_codes"))
-        res = [sb.tile([P, S], F32, name=f"res{c}", align_bytes=256) for c in range(M_TILES)]
+        res = {(c, a): sb.tile([P, HALF], F32, name="w1_bf1" if (c, a) == (0, 1) else f"res{c}{a}", align_bytes=256) for c in range(M_TILES) for a in range(2)}
         for c, j0, width in pieces:
             cols = slice(j0 % HALF, j0 % HALF + width)
             nc.tensor.matmul_mx(
                 out=acc[c, j0, width][:], lhsT=w1_mx[c][0][:].bitcast(FP8X4), lhsT_scale=w1_mx[c][1][:],
                 rhs=xw_got[j0 // HALF][:, cols].bitcast(FP8X4), rhs_scale=xs_plane[:, j0:j0 + width], start=False, stop=True)
-            if c == 1 and j0 % HALF == 0:
-                nc.vector.tensor_scalar(res[c][:, j0:j0 + width], acc[c, j0, width][:], thr_t[:, c, :], 0.0, ALU.add, ALU.max)
+            dst = res[c, j0 // HALF]
+            if j0 % HALF:
+                nc.vector.tensor_scalar(dst[:, cols], acc[c, j0, width][:], thr_t[:, c, :], 0.0, ALU.add, ALU.max)
             else:
-                nc.scalar.activation(res[c][:, j0:j0 + width], acc[c, j0, width][:], ACT.Relu, bias=thr_t[:, c, :])
-            if (j0 + width) % HALF == 0:
-                half = slice(j0 + width - HALF, j0 + width)
-                nc.sync.dma_start(out=out[c * P:(c + 1) * P, half], in_=res[c][:, half])
+                nc.scalar.activation(dst[:, cols], acc[c, j0, width][:], ACT.Relu, bias=thr_t[:, c, :])
+            if cols.stop == HALF:
+                nc.sync.dma_start(out=out[c * P:(c + 1) * P, j0 + width - HALF:j0 + width], in_=dst[:])

@@ -60,13 +60,13 @@ def tile_picked_ylista_nn_p_kernel(tc, x_words, x_scales, mem, w1, sr, thr, offs
         nc.sync.dma_start(out=sr_raw[:], in_=sr.rearrange("(p t) m -> p t m", t=PACK))
         nc.sync.dma_start(out=w1_raw[0][:], in_=w1_rows[:, :, 0:P])
         nc.vector.tensor_copy(xs_got[:], xs_win[:].indirect(offs_t[:]))
-        for q in range(4):
-            first = P - 16 + 4 * q
-            nc.gpsimd.dma_start(out=xs_plane[32 * q:32 * q + 4, :].bitcast(I32), in_=xs_got[first:first + 4, :].bitcast(I32))
 
         xw_win = sb.tile([P, T], I32, name="xw_win", align_bytes=256)
         nc.sync.dma_start(out=xw_win[:], in_=x_words[0].rearrange("p n t -> p (n t)").bitcast(I32))
         nc.sync.dma_start(out=w1_raw[1][:], in_=w1_rows[:, :, P:2 * P])
+        for q in range(4):
+            first = P - 16 + 4 * q
+            nc.sync.dma_start(out=xs_plane[32 * q:32 * q + 4, :].bitcast(I32), in_=xs_got[first:first + 4, :].bitcast(I32))
 
         h_bf = [sb.tile([P, HALF, PACK], BF16, name=f"h_bf{a}", align_bytes=256) for a in range(2)]
         pairs = [sb.tile([P, 2, S], BF16, name=f"pair{u}", align_bytes=256) for u in range(2)]

@@ -102,11 +102,6 @@ def tile_picked_ylista_nn_p_kernel(tc, x_words, x_scales, mem, w1, sr, thr, offs
         h_mx = [quantise(h_bf[a], HALF, f"h{a}", name) for a, name in enumerate(("h0_codes", "sr_bf1"))]
         w1_mx = [quantise(w1_bf[0], P, "w10", "w10_codes")]
 
-        warm = psum.tile([P, HALF], F32, name="acc7")
-        nc.tensor.matmul_mx(
-            out=warm[:], lhsT=h_mx[0][0][:, 0:P].bitcast(FP8X4), lhsT_scale=h_mx[0][1][:, 0:P],
-            rhs=h_mx[0][0][:].bitcast(FP8X4), rhs_scale=h_mx[0][1][:], start=True, stop=True)
-
         pieces = [(0, 0, HALF)] + [(0, j0, P) for j0 in range(HALF, S, P)] + [(1, j0, P) for j0 in range(0, S, P)]
         acc = {piece: psum.tile([P, piece[2]], F32, name=f"acc{i}") for i, piece in enumerate(pieces)}
         for c, j0, width in sorted(pieces, key=lambda piece: piece[1] // HALF):
@@ -115,6 +110,11 @@ def tile_picked_ylista_nn_p_kernel(tc, x_words, x_scales, mem, w1, sr, thr, offs
             nc.tensor.matmul_mx(
                 out=acc[c, j0, width][:], lhsT=sr_mx[c][0][:].bitcast(FP8X4), lhsT_scale=sr_mx[c][1][:],
                 rhs=codes[:, cols].bitcast(FP8X4), rhs_scale=scales[:, cols], start=True, stop=False)
+
+        warm = psum.tile([P, HALF], F32, name="acc7")
+        nc.tensor.matmul_mx(
+            out=warm[:], lhsT=w1_mx[0][0][:].bitcast(FP8X4), lhsT_scale=w1_mx[0][1][:],
+            rhs=h_mx[1][0][:].bitcast(FP8X4), rhs_scale=h_mx[1][1][:], start=True, stop=True)
 
         xw_got = [sb.tile([P, HALF], U32, name=f"xw_got{a}", align_bytes=256) for a in range(2)]
         for a in range(2):

@@ -111,11 +111,6 @@ def tile_picked_ylista_nn_p_kernel(tc, x_words, x_scales, mem, w1, sr, thr, offs
                 out=acc[c, j0, width][:], lhsT=sr_mx[c][0][:].bitcast(FP8X4), lhsT_scale=sr_mx[c][1][:],
                 rhs=codes[:, cols].bitcast(FP8X4), rhs_scale=scales[:, cols], start=True, stop=False)
 
-        warm = psum.tile([P, HALF], F32, name="acc7")
-        nc.tensor.matmul_mx(
-            out=warm[:], lhsT=w1_mx[0][0][:].bitcast(FP8X4), lhsT_scale=w1_mx[0][1][:],
-            rhs=h_mx[1][0][:].bitcast(FP8X4), rhs_scale=h_mx[1][1][:], start=True, stop=True)
-
         xw_got = [sb.tile([P, HALF], U32, name=f"xw_got{a}", align_bytes=256) for a in range(2)]
         for a in range(2):
             nc.vector.tensor_copy(xw_got[a][:], xw_win[:].bitcast(U32).indirect(offs_t[:, a * HALF // 16:(a + 1) * HALF // 16]))

@@ -28,79 +28,84 @@ def tile_picked_ylista_nn_p_kernel(tc, x_words, x_scales, mem, w1, sr, thr, offs
         sb = ctx.enter_context(tc.tile_pool(name="sb", bufs=1))
         psum = ctx.enter_context(tc.psum_pool(name="psum", bufs=1))
 
+        def tile(shape, dtype, name):
+            return sb.tile(shape, dtype, name=name, align_bytes=256)
+
         slot_t = sb.tile([P, S // 16], U16, name="slot_t")
         offs_t = sb.tile([P, S // 16], U16, name="offs_t")
-        xs_win = sb.tile([P, T], U8, name="xs_win", align_bytes=256)
-        xs_got = sb.tile([P, S], U8, name="xs_got", align_bytes=256)
-        xs_plane = sb.tile([P, S], U8, name="xs_plane", align_bytes=256)
-
+        xs_win = tile([P, T], U8, "xs_win")
+        xs_got = tile([P, S], U8, "xs_got")
+        xs_plane = tile([P, S], U8, "xs_plane")
         nc.vector.memset(xs_win[0:P - 16, :].bitcast(I32), 0)
         nc.vector.memset(xs_plane[:].bitcast(I32), 0)
 
         nc.scalar.dma_start(out=xs_win[P - 16:P, :].bitcast(I32), in_=x_scales[0].bitcast(I32))
         nc.sync.dma_start(offs_t[:], offs)
-        thr_rows = sb.tile([P, P], F32, name="thr_rows", align_bytes=256)
-        ident = sb.tile([P, P], F32, name="ident", align_bytes=256)
-        thr_t = sb.tile([P, M_TILES, 1], F32, name="thr_t", align_bytes=256)
+        nc.sync.dma_start(slot_t[:], slot)
         mem_rows = mem.rearrange("(p t) u -> p t u", t=PACK)
-        mem_t = [sb.tile([P, U], F32, name=f"mem{t}", align_bytes=256) for t in range(PACK)]
-        for t in range(PACK):
-            nc.sync.dma_start(out=mem_t[t][:], in_=mem_rows[:, t, :])
-            if t == 0:
-                nc.sync.dma_start(slot_t[:], slot)
+        mem_t = [tile([P, 2, U], F32, f"mem{u}") for u in range(2)]
+        for u in range(2):
+            nc.sync.dma_start(out=mem_t[u][:], in_=mem_rows[:, 2 * u:2 * u + 2, :])
+        thr_rows = tile([P, P], F32, "thr_rows")
+        ident = tile([P, P], F32, "ident")
+        thr_t = tile([P, M_TILES, 1], F32, "thr_t")
         nc.sync.dma_start(out=thr_rows[P - M_TILES:P, :], in_=thr.rearrange("(c p) o -> c (p o)", p=P))
         nc.gpsimd.memset(thr_rows[0:P - M_TILES, :], 0.0)
         make_identity(nc, ident[:])
-        thr_ps = psum.tile([P, P], F32, name="acc7")
+        thr_ps = psum.tile([P, P], F32, name="thr_ps")
         nc.tensor.transpose(thr_ps[:], thr_rows[:], ident[:])
         nc.scalar.activation(thr_t[:, :, 0], thr_ps[:, P - M_TILES:P], ACT.Copy)
-        sr_raw = sb.tile([P, PACK, N], F32, name="sr_raw", align_bytes=256)
-        w1_raw = [sb.tile([P, PACK, P], F32, name=f"w1_raw{c}", align_bytes=256) for c in range(M_TILES)]
+        sr_raw = tile([P, PACK, N], F32, "sr_raw")
+        w1_raw = [tile([P, PACK, P], F32, f"w1_raw{c}") for c in range(M_TILES)]
         w1_rows = w1.rearrange("(p t) m -> p t m", t=PACK)
         nc.sync.dma_start(out=sr_raw[:], in_=sr.rearrange("(p t) m -> p t m", t=PACK))
         nc.sync.dma_start(out=w1_raw[0][:], in_=w1_rows[:, :, 0:P])
         nc.vector.tensor_copy(xs_got[:], xs_win[:].indirect(offs_t[:]))
-
-        xw_win = sb.tile([P, T], I32, name="xw_win", align_bytes=256)
+        xw_win = tile([P, T], I32, "xw_win")
         nc.sync.dma_start(out=xw_win[:], in_=x_words[0].rearrange("p n t -> p (n t)").bitcast(I32))
         nc.sync.dma_start(out=w1_raw[1][:], in_=w1_rows[:, :, P:2 * P])
         for q in range(4):
             first = P - 16 + 4 * q
             nc.sync.dma_start(out=xs_plane[32 * q:32 * q + 4, :].bitcast(I32), in_=xs_got[first:first + 4, :].bitcast(I32))
 
-        h_bf = [sb.tile([P, HALF, PACK], BF16, name=f"h_bf{a}", align_bytes=256) for a in range(2)]
-        pairs = [sb.tile([P, 2, S], BF16, name=f"pair{u}", align_bytes=256) for u in range(2)]
-        for t in range(PACK - 1):
-            nc.vector.tensor_copy(pairs[t // 2][:, t % 2, :], mem_t[t][:].indirect(slot_t[:]))
-        for a in range(2):
-            nc.vector.tensor_copy(pairs[1][:, 1, a * HALF:(a + 1) * HALF], mem_t[PACK - 1][:].indirect(slot_t[:, a * HALF // 16:(a + 1) * HALF // 16]))
-        for a in range(2):
-            cols = slice(a * HALF, (a + 1) * HALF)
-            nc.scalar.activation(h_bf[a][:, :, 0:2], pairs[0][:, :, cols].rearrange("p t c -> p c t"), ACT.Copy)
-        for a in range(2):
-            cols = slice(a * HALF, (a + 1) * HALF)
-            src = pairs[1][:, :, cols].rearrange("p t c -> p c t")
-            nc.vector.tensor_copy(h_bf[a][:, :, 2:4], src)
+        def half_of(list_t, a):
+            return list_t[:, a * HALF // 16:(a + 1) * HALF // 16]
+
+        pairs = [tile([P, 2, HALF, 2], BF16, f"pairs{a}") for a in range(2)]
+        for u in range(2):
+            for a in range(2):
+                for e in range(2):
+                    nc.vector.tensor_copy(pairs[a][:, u, :, e], mem_t[u][:, e, :].indirect(half_of(slot_t, a)))
+
+        def weave(a, name):
+            woven = tile([P, HALF, PACK], BF16, name)
+            words = pairs[a][:].rearrange("p u c e -> p u (c e)").bitcast(U32)
+            nc.scalar.copy(woven[:].rearrange("p c t -> p (c t)").bitcast(U32).rearrange("p (c u) -> p c u", u=2), words.rearrange("p u c -> p c u"))
+            return woven
 
         def interleave(grouped, raw, cols):
             return grouped[:, cols, :].rearrange("p (c i) t -> p c t i", i=4), raw[:, :, cols].rearrange("p t (c i) -> p c t i", i=4)
 
         def quantise(grouped, width, name, codes_name):
-            codes = sb.tile([P, width], U32, name=codes_name, align_bytes=256)
-            scales = sb.tile([P, width], U8, name=name + "_scales", align_bytes=256)
+            codes = tile([P, width], U32, codes_name)
+            scales = tile([P, width], U8, name + "_scales")
             nc.vector.quantize_mx(out=codes[:].bitcast(FP8X4), scales=scales[:], in_=grouped[:].rearrange("p c t -> p (c t)"))
             return codes, scales
 
-        sr_bf = [sb.tile([P, P, PACK], BF16, name=f"sr_bf{c}", align_bytes=256) for c in range(M_TILES)]
-        w1_bf = [sb.tile([P, P, PACK], BF16, name=f"w1_bf{c}", align_bytes=256) for c in range(M_TILES)]
-        for c in range(M_TILES):
-            nc.scalar.activation(*interleave(sr_bf[c], sr_raw[:, :, c * P:(c + 1) * P], slice(0, P)), ACT.Copy)
-        nc.scalar.activation(*interleave(w1_bf[0], w1_raw[0], slice(0, P)), ACT.Copy)
+        sr_bf = [tile([P, P, PACK], BF16, f"sr_bf{c}") for c in range(M_TILES)]
+        w1_bf = [tile([P, P, PACK], BF16, f"w1_bf{c}") for c in range(M_TILES)]
+        h_bf = [weave(0, "h_bf0")]
+        nc.scalar.activation(*interleave(sr_bf[0], sr_raw[:, :, 0:P], slice(0, P)), ACT.Copy)
+        nc.scalar.activation(*interleave(sr_bf[1], sr_raw[:, :, P:2 * P], slice(0, P // 2)), ACT.Copy)
+        nc.gpsimd.tensor_scalar(*interleave(sr_bf[1], sr_raw[:, :, P:2 * P], slice(P // 2, P)), 1.0, 0.0, ALU.mult, ALU.add)
+        nc.vector.tensor_copy(*interleave(w1_bf[0], w1_raw[0], slice(0, P)))
+        h_bf.append(weave(1, "sr_raw"))
         nc.scalar.activation(*interleave(w1_bf[1], w1_raw[1], slice(0, 3 * P // 4)), ACT.Copy)
         nc.gpsimd.tensor_scalar(*interleave(w1_bf[1], w1_raw[1], slice(3 * P // 4, P)), 1.0, 0.0, ALU.mult, ALU.add)
+        h_mx = [quantise(h_bf[0], HALF, "h0", "h0_codes")]
         sr_mx = [quantise(sr_bf[c], P, f"sr{c}", f"sr{c}_codes") for c in range(M_TILES)]
-        h_mx = [quantise(h_bf[a], HALF, f"h{a}", name) for a, name in enumerate(("h0_codes", "sr_bf1"))]
         w1_mx = [quantise(w1_bf[0], P, "w10", "w10_codes")]
+        h_mx.append(quantise(h_bf[1], HALF, "h1", "h1_codes"))
 
         pieces = [(0, 0, HALF)] + [(0, j0, P) for j0 in range(HALF, S, P)] + [(1, j0, P) for j0 in range(0, S, P)]
         acc = {piece: psum.tile([P, piece[2]], F32, name=f"acc{i}") for i, piece in enumerate(pieces)}
@@ -111,11 +116,11 @@ def tile_picked_ylista_nn_p_kernel(tc, x_words, x_scales, mem, w1, sr, thr, offs
                 out=acc[c, j0, width][:], lhsT=sr_mx[c][0][:].bitcast(FP8X4), lhsT_scale=sr_mx[c][1][:],
                 rhs=codes[:, cols].bitcast(FP8X4), rhs_scale=scales[:, cols], start=True, stop=False)
 
-        xw_got = [sb.tile([P, HALF], U32, name=f"xw_got{a}", align_bytes=256) for a in range(2)]
+        xw_got = [tile([P, HALF], U32, f"pairs{1 - a}") for a in range(2)]
         for a in range(2):
-            nc.vector.tensor_copy(xw_got[a][:], xw_win[:].bitcast(U32).indirect(offs_t[:, a * HALF // 16:(a + 1) * HALF // 16]))
+            nc.vector.tensor_copy(xw_got[a][:], xw_win[:].bitcast(U32).indirect(half_of(offs_t, a)))
         w1_mx.append(quantise(w1_bf[1], P, "w11", "w11_codes"))
-        res = {(c, a): sb.tile([P, HALF], F32, name="w1_bf1" if (c, a) == (0, 1) else f"res{c}{a}", align_bytes=256) for c in range(M_TILES) for a in range(2)}
+        res = {(c, a): tile([P, HALF], F32, "w1_bf1" if (c, a) == (0, 1) else f"res{c}{a}") for c in range(M_TILES) for a in range(2)}
         for c, j0, width in pieces:
             cols = slice(j0 % HALF, j0 % HALF + width)
             nc.tensor.matmul_mx(

@@ -41,11 +41,12 @@ def tile_picked_ylista_nn_p_kernel(tc, x_words, x_scales, mem, w1, sr, thr, offs
 
         nc.scalar.dma_start(out=xs_win[P - 16:P, :].bitcast(I32), in_=x_scales[0].bitcast(I32))
         nc.sync.dma_start(offs_t[:], offs)
-        nc.sync.dma_start(slot_t[:], slot)
         mem_rows = mem.rearrange("(p t) u -> p t u", t=PACK)
-        mem_t = [tile([P, 2, U], F32, f"mem{u}") for u in range(2)]
-        for u in range(2):
-            nc.sync.dma_start(out=mem_t[u][:], in_=mem_rows[:, 2 * u:2 * u + 2, :])
+        mem_t = [tile([P, U], F32, f"mem{t}") for t in range(PACK)]
+        for t in range(PACK):
+            nc.sync.dma_start(out=mem_t[t][:], in_=mem_rows[:, t, :])
+            if t == 0:
+                nc.sync.dma_start(slot_t[:], slot)
         thr_rows = tile([P, P], F32, "thr_rows")
         ident = tile([P, P], F32, "ident")
         thr_t = tile([P, M_TILES, 1], F32, "thr_t")
@@ -71,16 +72,15 @@ def tile_picked_ylista_nn_p_kernel(tc, x_words, x_scales, mem, w1, sr, thr, offs
         def half_of(list_t, a):
             return list_t[:, a * HALF // 16:(a + 1) * HALF // 16]
 
-        pairs = [tile([P, 2, HALF, 2], BF16, f"pairs{a}") for a in range(2)]
-        for u in range(2):
-            for a in range(2):
-                for e in range(2):
-                    nc.vector.tensor_copy(pairs[a][:, u, :, e], mem_t[u][:, e, :].indirect(half_of(slot_t, a)))
+        pairs = tile([P, 2, S, 2], BF16, "pairs")
+        for t in range(PACK):
+            nc.vector.tensor_copy(pairs[:, t // 2, :, t % 2], mem_t[t][:].indirect(slot_t[:]))
+        words = pairs[:].rearrange("p u c e -> p u (c e)").bitcast(I32).rearrange("p u c -> p c u")
 
-        def weave(a, name):
-            woven = tile([P, HALF, PACK], BF16, name)
-            words = pairs[a][:].rearrange("p u c e -> p u (c e)").bitcast(U32)
-            nc.scalar.copy(woven[:].rearrange("p c t -> p (c t)").bitcast(U32).rearrange("p (c u) -> p c u", u=2), words.rearrange("p u c -> p c u"))
+        def weave(a):
+            woven = tile([P, HALF, PACK], BF16, f"h_bf{a}")
+            dst = woven[:].rearrange("p c t -> p (c t)").bitcast(I32).rearrange("p (c u) -> p c u", u=2)
+            nc.vector.tensor_copy(dst, words[:, a * HALF:(a + 1) * HALF, :])
             return woven
 
         def interleave(grouped, raw, cols):
@@ -94,18 +94,15 @@ def tile_picked_ylista_nn_p_kernel(tc, x_words, x_scales, mem, w1, sr, thr, offs
 
         sr_bf = [tile([P, P, PACK], BF16, f"sr_bf{c}") for c in range(M_TILES)]
         w1_bf = [tile([P, P, PACK], BF16, f"w1_bf{c}") for c in range(M_TILES)]
-        h_bf = [weave(0, "h_bf0")]
-        nc.scalar.activation(*interleave(sr_bf[0], sr_raw[:, :, 0:P], slice(0, P)), ACT.Copy)
-        nc.scalar.activation(*interleave(sr_bf[1], sr_raw[:, :, P:2 * P], slice(0, P // 2)), ACT.Copy)
-        nc.gpsimd.tensor_scalar(*interleave(sr_bf[1], sr_raw[:, :, P:2 * P], slice(P // 2, P)), 1.0, 0.0, ALU.mult, ALU.add)
-        nc.vector.tensor_copy(*interleave(w1_bf[0], w1_raw[0], slice(0, P)))
-        h_bf.append(weave(1, "sr_raw"))
+        h_bf = [weave(a) for a in range(2)]
+        for c in range(M_TILES):
+            nc.scalar.activation(*interleave(sr_bf[c], sr_raw[:, :, c * P:(c + 1) * P], slice(0, P)), ACT.Copy)
+        nc.scalar.activation(*interleave(w1_bf[0], w1_raw[0], slice(0, P)), ACT.Copy)
         nc.scalar.activation(*interleave(w1_bf[1], w1_raw[1], slice(0, 3 * P // 4)), ACT.Copy)
         nc.gpsimd.tensor_scalar(*interleave(w1_bf[1], w1_raw[1], slice(3 * P // 4, P)), 1.0, 0.0, ALU.mult, ALU.add)
-        h_mx = [quantise(h_bf[0], HALF, "h0", "h0_codes")]
         sr_mx = [quantise(sr_bf[c], P, f"sr{c}", f"sr{c}_codes") for c in range(M_TILES)]
+        h_mx = [quantise(h_bf[a], HALF, f"h{a}", f"h{a}_codes") for a in range(2)]
         w1_mx = [quantise(w1_bf[0], P, "w10", "w10_codes")]
-        h_mx.append(quantise(h_bf[1], HALF, "h1", "h1_codes"))
 
         pieces = [(0, 0, HALF)] + [(0, j0, P) for j0 in range(HALF, S, P)] + [(1, j0, P) for j0 in range(0, S, P)]
         acc = {piece: psum.tile([P, piece[2]], F32, name=f"acc{i}") for i, piece in enumerate(pieces)}
@@ -116,7 +113,7 @@ def tile_picked_ylista_nn_p_kernel(tc, x_words, x_scales, mem, w1, sr, thr, offs
                 out=acc[c, j0, width][:], lhsT=sr_mx[c][0][:].bitcast(FP8X4), lhsT_scale=sr_mx[c][1][:],
                 rhs=codes[:, cols].bitcast(FP8X4), rhs_scale=scales[:, cols], start=True, stop=False)
 
-        xw_got = [tile([P, HALF], U32, f"pairs{1 - a}") for a in range(2)]
+        xw_got = [tile([P, HALF], U32, f"xw_got{a}") for a in range(2)]
         for a in range(2):
             nc.vector.tensor_copy(xw_got[a][:], xw_win[:].bitcast(U32).indirect(half_of(offs_t, a)))
         w1_mx.append(quantise(w1_bf[1], P, "w11", "w11_codes"))

@@ -72,16 +72,16 @@ def tile_picked_ylista_nn_p_kernel(tc, x_words, x_scales, mem, w1, sr, thr, offs
         def half_of(list_t, a):
             return list_t[:, a * HALF // 16:(a + 1) * HALF // 16]
 
-        pairs = tile([P, 2, S, 2], BF16, "pairs")
-        for t in range(PACK):
-            nc.vector.tensor_copy(pairs[:, t // 2, :, t % 2], mem_t[t][:].indirect(slot_t[:]))
-        words = pairs[:].rearrange("p u c e -> p u (c e)").bitcast(I32).rearrange("p u c -> p c u")
+        pairs = tile([P, 2, 2, HALF, 2], BF16, "pairs")
+        for t in range(PACK - 1):
+            nc.vector.tensor_copy(pairs[:, :, t // 2, :, t % 2], mem_t[t][:].indirect(slot_t[:]))
+        for a in range(2):
+            nc.vector.tensor_copy(pairs[:, a, 1, :, 1], mem_t[PACK - 1][:].indirect(half_of(slot_t, a)))
 
-        def weave(a):
-            woven = tile([P, HALF, PACK], BF16, f"h_bf{a}")
-            dst = woven[:].rearrange("p c t -> p (c t)").bitcast(I32).rearrange("p (c u) -> p c u", u=2)
-            nc.vector.tensor_copy(dst, words[:, a * HALF:(a + 1) * HALF, :])
-            return woven
+        def weave(a, name, dtype):
+            woven = tile([P, HALF, PACK], BF16, name)
+            dst = woven[:].rearrange("p c t -> p (c t)").bitcast(dtype).rearrange("p (c u) -> p c u", u=2)
+            return woven, dst, pairs[:, a].rearrange("p u c e -> p u (c e)").bitcast(dtype).rearrange("p u c -> p c u")
 
         def interleave(grouped, raw, cols):
             return grouped[:, cols, :].rearrange("p (c i) t -> p c t i", i=4), raw[:, :, cols].rearrange("p t (c i) -> p c t i", i=4)
@@ -94,14 +94,18 @@ def tile_picked_ylista_nn_p_kernel(tc, x_words, x_scales, mem, w1, sr, thr, offs
 
         sr_bf = [tile([P, P, PACK], BF16, f"sr_bf{c}") for c in range(M_TILES)]
         w1_bf = [tile([P, P, PACK], BF16, f"w1_bf{c}") for c in range(M_TILES)]
-        h_bf = [weave(a) for a in range(2)]
-        for c in range(M_TILES):
-            nc.scalar.activation(*interleave(sr_bf[c], sr_raw[:, :, c * P:(c + 1) * P], slice(0, P)), ACT.Copy)
+        h0_bf, dst, src = weave(0, "h_bf0", I32)
+        nc.vector.tensor_copy(dst, src)
+        nc.scalar.activation(*interleave(sr_bf[0], sr_raw[:, :, 0:P], slice(0, P)), ACT.Copy)
+        nc.scalar.activation(*interleave(sr_bf[1], sr_raw[:, :, P:2 * P], slice(0, P // 2)), ACT.Copy)
+        nc.gpsimd.tensor_scalar(*interleave(sr_bf[1], sr_raw[:, :, P:2 * P], slice(P // 2, P)), 1.0, 0.0, ALU.mult, ALU.add)
+        h1_bf, dst, src = weave(1, "sr_raw", U32)
+        nc.scalar.copy(dst, src)
         nc.scalar.activation(*interleave(w1_bf[0], w1_raw[0], slice(0, P)), ACT.Copy)
         nc.scalar.activation(*interleave(w1_bf[1], w1_raw[1], slice(0, 3 * P // 4)), ACT.Copy)
         nc.gpsimd.tensor_scalar(*interleave(w1_bf[1], w1_raw[1], slice(3 * P // 4, P)), 1.0, 0.0, ALU.mult, ALU.add)
         sr_mx = [quantise(sr_bf[c], P, f"sr{c}", f"sr{c}_codes") for c in range(M_TILES)]
-        h_mx = [quantise(h_bf[a], HALF, f"h{a}", f"h{a}_codes") for a in range(2)]
+        h_mx = [quantise(h_bf, HALF, f"h{a}", f"h{a}_codes") for a, h_bf in enumerate((h0_bf, h1_bf))]
         w1_mx = [quantise(w1_bf[0], P, "w10", "w10_codes")]
 
         pieces = [(0, 0, HALF)] + [(0, j0, P) for j0 in range(HALF, S, P)] + [(1, j0, P) for j0 in range(0, S, P)]
@@ -113,18 +117,23 @@ def tile_picked_ylista_nn_p_kernel(tc, x_words, x_scales, mem, w1, sr, thr, offs
                 out=acc[c, j0, width][:], lhsT=sr_mx[c][0][:].bitcast(FP8X4), lhsT_scale=sr_mx[c][1][:],
                 rhs=codes[:, cols].bitcast(FP8X4), rhs_scale=scales[:, cols], start=True, stop=False)
 
+        warm = psum.tile([P, HALF], F32, name="thr_ps")
+        nc.tensor.matmul_mx(
+            out=warm[:], lhsT=sr_mx[1][0][:].bitcast(FP8X4), lhsT_scale=sr_mx[1][1][:],
+            rhs=h_mx[1][0][:].bitcast(FP8X4), rhs_scale=h_mx[1][1][:], start=True, stop=True)
+
         xw_got = [tile([P, HALF], U32, f"xw_got{a}") for a in range(2)]
         for a in range(2):
             nc.vector.tensor_copy(xw_got[a][:], xw_win[:].bitcast(U32).indirect(half_of(offs_t, a)))
         w1_mx.append(quantise(w1_bf[1], P, "w11", "w11_codes"))
-        res = {(c, a): tile([P, HALF], F32, "w1_bf1" if (c, a) == (0, 1) else f"res{c}{a}") for c in range(M_TILES) for a in range(2)}
+        res = {(c, a): tile([P, HALF], F32, f"res{c}{a}") for c in range(M_TILES) for a in range(2)}
         for c, j0, width in pieces:
             cols = slice(j0 % HALF, j0 % HALF + width)
             nc.tensor.matmul_mx(
                 out=acc[c, j0, width][:], lhsT=w1_mx[c][0][:].bitcast(FP8X4), lhsT_scale=w1_mx[c][1][:],
                 rhs=xw_got[j0 // HALF][:, cols].bitcast(FP8X4), rhs_scale=xs_plane[:, j0:j0 + width], start=False, stop=True)
             dst = res[c, j0 // HALF]
-            if j0 % HALF:
+            if c == 1 and j0 != HALF:
                 nc.vector.tensor_scalar(dst[:, cols], acc[c, j0, width][:], thr_t[:, c, :], 0.0, ALU.add, ALU.max)
             else:
                 nc.scalar.activation(dst[:, cols], acc[c, j0, width][:], ACT.Relu, bias=thr_t[:, c, :])

@@ -102,8 +102,8 @@ def tile_picked_ylista_nn_p_kernel(tc, x_words, x_scales, mem, w1, sr, thr, offs
         h1_bf, dst, src = weave(1, "sr_raw", U32)
         nc.scalar.copy(dst, src)
         nc.scalar.activation(*interleave(w1_bf[0], w1_raw[0], slice(0, P)), ACT.Copy)
-        nc.scalar.activation(*interleave(w1_bf[1], w1_raw[1], slice(0, 3 * P // 4)), ACT.Copy)
-        nc.gpsimd.tensor_scalar(*interleave(w1_bf[1], w1_raw[1], slice(3 * P // 4, P)), 1.0, 0.0, ALU.mult, ALU.add)
+        nc.scalar.activation(*interleave(w1_bf[1], w1_raw[1], slice(0, 5 * P // 8)), ACT.Copy)
+        nc.gpsimd.tensor_scalar(*interleave(w1_bf[1], w1_raw[1], slice(5 * P // 8, P)), 1.0, 0.0, ALU.mult, ALU.add)
         sr_mx = [quantise(sr_bf[c], P, f"sr{c}", f"sr{c}_codes") for c in range(M_TILES)]
         h_mx = [quantise(h_bf, HALF, f"h{a}", f"h{a}_codes") for a, h_bf in enumerate((h0_bf, h1_bf))]
         w1_mx = [quantise(w1_bf[0], P, "w10", "w10_codes")]
@@ -126,14 +126,14 @@ def tile_picked_ylista_nn_p_kernel(tc, x_words, x_scales, mem, w1, sr, thr, offs
         for a in range(2):
             nc.vector.tensor_copy(xw_got[a][:], xw_win[:].bitcast(U32).indirect(half_of(offs_t, a)))
         w1_mx.append(quantise(w1_bf[1], P, "w11", "w11_codes"))
-        res = {(c, a): tile([P, HALF], F32, f"res{c}{a}") for c in range(M_TILES) for a in range(2)}
+        res = {(c, a): tile([P, HALF], F32, "w1_bf1" if (c, a) == (0, 1) else f"res{c}{a}") for c in range(M_TILES) for a in range(2)}
         for c, j0, width in pieces:
             cols = slice(j0 % HALF, j0 % HALF + width)
             nc.tensor.matmul_mx(
                 out=acc[c, j0, width][:], lhsT=w1_mx[c][0][:].bitcast(FP8X4), lhsT_scale=w1_mx[c][1][:],
                 rhs=xw_got[j0 // HALF][:, cols].bitcast(FP8X4), rhs_scale=xs_plane[:, j0:j0 + width], start=False, stop=True)
             dst = res[c, j0 // HALF]
-            if c == 1 and j0 != HALF:
+            if j0 % HALF:
                 nc.vector.tensor_scalar(dst[:, cols], acc[c, j0, width][:], thr_t[:, c, :], 0.0, ALU.add, ALU.max)
             else:
                 nc.scalar.activation(dst[:, cols], acc[c, j0, width][:], ACT.Relu, bias=thr_t[:, c, :])

@@ -20,6 +20,8 @@ P = 128
 PACK = 4
 HALF = S // 2
 M_TILES = N // P
+SCALE_ROWS = 16
+QUARTER = S // 4
 
 
 def tile_picked_ylista_nn_p_kernel(tc, x_words, x_scales, mem, w1, sr, thr, offs, slot, out):
@@ -36,106 +38,98 @@ def tile_picked_ylista_nn_p_kernel(tc, x_words, x_scales, mem, w1, sr, thr, offs
         xs_win = tile([P, T], U8, "xs_win")
         xs_got = tile([P, S], U8, "xs_got")
         xs_plane = tile([P, S], U8, "xs_plane")
-        nc.vector.memset(xs_win[0:P - 16, :].bitcast(I32), 0)
+        thr_rows = tile([P, P], F32, "thr_rows")
+        nc.vector.memset(thr_rows[0:P - M_TILES, 0:P // 2], 0.0)
+        nc.scalar.activation(thr_rows[0:P - M_TILES, P // 2:P], thr_rows[0:P - M_TILES, 0:P // 2], ACT.Copy)
+        nc.vector.memset(xs_win[0:P - SCALE_ROWS, :].bitcast(I32), 0)
         nc.vector.memset(xs_plane[:].bitcast(I32), 0)
 
-        nc.scalar.dma_start(out=xs_win[P - 16:P, :].bitcast(I32), in_=x_scales[0].bitcast(I32))
+        nc.scalar.dma_start(out=xs_win[P - SCALE_ROWS:P, :].bitcast(I32), in_=x_scales[0].bitcast(I32))
         nc.sync.dma_start(offs_t[:], offs)
         mem_rows = mem.rearrange("(p t) u -> p t u", t=PACK)
-        mem_t = [tile([P, U], F32, f"mem{t}") for t in range(PACK)]
-        for t in range(PACK):
-            nc.sync.dma_start(out=mem_t[t][:], in_=mem_rows[:, t, :])
-            if t == 0:
-                nc.sync.dma_start(slot_t[:], slot)
-        thr_rows = tile([P, P], F32, "thr_rows")
+        mem_t = [tile([P, 2, U], F32, f"mem{u}") for u in range(2)]
+        nc.sync.dma_start(out=mem_t[0][:], in_=mem_rows[:, 0:2, :])
+        nc.sync.dma_start(slot_t[:], slot)
+        nc.sync.dma_start(out=mem_t[1][:], in_=mem_rows[:, 2:4, :])
         ident = tile([P, P], F32, "ident")
         thr_t = tile([P, M_TILES, 1], F32, "thr_t")
         nc.sync.dma_start(out=thr_rows[P - M_TILES:P, :], in_=thr.rearrange("(c p) o -> c (p o)", p=P))
-        nc.gpsimd.memset(thr_rows[0:P - M_TILES, :], 0.0)
         make_identity(nc, ident[:])
         thr_ps = psum.tile([P, P], F32, name="thr_ps")
         nc.tensor.transpose(thr_ps[:], thr_rows[:], ident[:])
-        nc.scalar.activation(thr_t[:, :, 0], thr_ps[:, P - M_TILES:P], ACT.Copy)
-        sr_raw = tile([P, PACK, N], F32, "sr_raw")
-        w1_raw = [tile([P, PACK, P], F32, f"w1_raw{c}") for c in range(M_TILES)]
-        w1_rows = w1.rearrange("(p t) m -> p t m", t=PACK)
-        nc.sync.dma_start(out=sr_raw[:], in_=sr.rearrange("(p t) m -> p t m", t=PACK))
-        nc.sync.dma_start(out=w1_raw[0][:], in_=w1_rows[:, :, 0:P])
+
+        def load_weights(weights, name):
+            raw = tile([P, PACK, N], F32, name)
+            nc.sync.dma_start(out=raw[:], in_=weights.rearrange("(p t) m -> p t m", t=PACK))
+            return raw
+
         nc.vector.tensor_copy(xs_got[:], xs_win[:].indirect(offs_t[:]))
+        sr_raw = load_weights(sr, "sr_raw")
+        w1_raw = load_weights(w1, "w1_raw")
         xw_win = tile([P, T], I32, "xw_win")
         nc.sync.dma_start(out=xw_win[:], in_=x_words[0].rearrange("p n t -> p (n t)").bitcast(I32))
-        nc.sync.dma_start(out=w1_raw[1][:], in_=w1_rows[:, :, P:2 * P])
         for q in range(4):
-            first = P - 16 + 4 * q
-            nc.sync.dma_start(out=xs_plane[32 * q:32 * q + 4, :].bitcast(I32), in_=xs_got[first:first + 4, :].bitcast(I32))
+            first = P - SCALE_ROWS + 4 * q
+            queue = nc.gpsimd if q == 0 else nc.sync
+            queue.dma_start(out=xs_plane[32 * q:32 * q + 4, :].bitcast(I32), in_=xs_got[first:first + 4, :].bitcast(I32))
 
-        def half_of(list_t, a):
-            return list_t[:, a * HALF // 16:(a + 1) * HALF // 16]
+        def entries(list_t, j0, width):
+            return list_t[:, j0 // 16:(j0 + width) // 16]
 
-        pairs = tile([P, 2, 2, HALF, 2], BF16, "pairs")
-        for t in range(PACK - 1):
-            nc.vector.tensor_copy(pairs[:, :, t // 2, :, t % 2], mem_t[t][:].indirect(slot_t[:]))
-        for a in range(2):
-            nc.vector.tensor_copy(pairs[:, a, 1, :, 1], mem_t[PACK - 1][:].indirect(half_of(slot_t, a)))
+        pairs = tile([P, 2, HALF, 2], BF16, "pairs")
+        planes = tile([P, PACK, HALF], F32, "planes")
+        for t in range(PACK):
+            window = mem_t[t // 2][:, t % 2, :]
+            nc.vector.tensor_copy(pairs[:, t // 2, :, t % 2], window.indirect(entries(slot_t, 0, HALF)))
+            nc.scalar.activation(planes[:, t, :], window.indirect(entries(slot_t, HALF, HALF)), ACT.Copy)
 
-        def weave(a, name, dtype):
-            woven = tile([P, HALF, PACK], BF16, name)
-            dst = woven[:].rearrange("p c t -> p (c t)").bitcast(dtype).rearrange("p (c u) -> p c u", u=2)
-            return woven, dst, pairs[:, a].rearrange("p u c e -> p u (c e)").bitcast(dtype).rearrange("p u c -> p c u")
+        def interleave(grouped, raw):
+            return grouped[:].rearrange("p (c i) t -> p c t i", i=4), raw[:].rearrange("p t (c i) -> p c t i", i=4)
 
-        def interleave(grouped, raw, cols):
-            return grouped[:, cols, :].rearrange("p (c i) t -> p c t i", i=4), raw[:, :, cols].rearrange("p t (c i) -> p c t i", i=4)
-
-        def quantise(grouped, width, name, codes_name):
-            codes = tile([P, width], U32, codes_name)
+        def quantise(grouped, width, name):
+            codes = tile([P, width], U32, name + "_codes")
             scales = tile([P, width], U8, name + "_scales")
             nc.vector.quantize_mx(out=codes[:].bitcast(FP8X4), scales=scales[:], in_=grouped[:].rearrange("p c t -> p (c t)"))
             return codes, scales
 
-        sr_bf = [tile([P, P, PACK], BF16, f"sr_bf{c}") for c in range(M_TILES)]
-        w1_bf = [tile([P, P, PACK], BF16, f"w1_bf{c}") for c in range(M_TILES)]
-        h0_bf, dst, src = weave(0, "h_bf0", I32)
-        nc.vector.tensor_copy(dst, src)
-        nc.scalar.activation(*interleave(sr_bf[0], sr_raw[:, :, 0:P], slice(0, P)), ACT.Copy)
-        nc.scalar.activation(*interleave(sr_bf[1], sr_raw[:, :, P:2 * P], slice(0, P // 2)), ACT.Copy)
-        nc.gpsimd.tensor_scalar(*interleave(sr_bf[1], sr_raw[:, :, P:2 * P], slice(P // 2, P)), 1.0, 0.0, ALU.mult, ALU.add)
-        h1_bf, dst, src = weave(1, "sr_raw", U32)
-        nc.scalar.copy(dst, src)
-        nc.scalar.activation(*interleave(w1_bf[0], w1_raw[0], slice(0, P)), ACT.Copy)
-        nc.scalar.activation(*interleave(w1_bf[1], w1_raw[1], slice(0, 5 * P // 8)), ACT.Copy)
-        nc.gpsimd.tensor_scalar(*interleave(w1_bf[1], w1_raw[1], slice(5 * P // 8, P)), 1.0, 0.0, ALU.mult, ALU.add)
-        sr_mx = [quantise(sr_bf[c], P, f"sr{c}", f"sr{c}_codes") for c in range(M_TILES)]
-        h_mx = [quantise(h_bf, HALF, f"h{a}", f"h{a}_codes") for a, h_bf in enumerate((h0_bf, h1_bf))]
-        w1_mx = [quantise(w1_bf[0], P, "w10", "w10_codes")]
+        h_bf = [tile([P, HALF, PACK], BF16, f"h_bf{a}") for a in range(2)]
+        nc.vector.tensor_copy(
+            h_bf[0][:].rearrange("p c t -> p (c t)").bitcast(I32).rearrange("p (c u) -> p c u", u=2),
+            pairs[:].rearrange("p u c e -> p u (c e)").bitcast(I32).rearrange("p u c -> p c u"))
+        nc.vector.tensor_copy(*interleave(h_bf[1], planes))
+        sr_bf = tile([P, N, PACK], BF16, "sr_bf")
+        w1_bf = tile([P, N, PACK], BF16, "w1_bf")
+        nc.scalar.activation(*interleave(sr_bf, sr_raw), ACT.Copy)
+        nc.scalar.activation(thr_t[:, :, 0], thr_ps[:, P - M_TILES:P], ACT.Copy)
+        nc.scalar.activation(*interleave(w1_bf, w1_raw), ACT.Copy)
+        h_mx = [quantise(h_bf[a], HALF, f"h{a}") for a in range(2)]
+        sr_codes, sr_scales = quantise(sr_bf, N, "sr")
+        w1_codes, w1_scales = quantise(w1_bf, N, "w1")
 
-        pieces = [(0, 0, HALF)] + [(0, j0, P) for j0 in range(HALF, S, P)] + [(1, j0, P) for j0 in range(0, S, P)]
-        acc = {piece: psum.tile([P, piece[2]], F32, name=f"acc{i}") for i, piece in enumerate(pieces)}
-        for c, j0, width in sorted(pieces, key=lambda piece: piece[1] // HALF):
+        stretches = [(j0, QUARTER) for j0 in range(0, S, QUARTER)]
+        acc = {(j0, c): psum.tile([P, width], F32, name="thr_ps" if (j0, c) == (S - QUARTER, M_TILES - 1) else f"acc{j0}_{c}") for j0, width in stretches for c in range(M_TILES)}
+        for j0, width in stretches:
             cols = slice(j0 % HALF, j0 % HALF + width)
             codes, scales = h_mx[j0 // HALF]
-            nc.tensor.matmul_mx(
-                out=acc[c, j0, width][:], lhsT=sr_mx[c][0][:].bitcast(FP8X4), lhsT_scale=sr_mx[c][1][:],
-                rhs=codes[:, cols].bitcast(FP8X4), rhs_scale=scales[:, cols], start=True, stop=False)
+            for c in range(M_TILES):
+                rows = slice(c * P, (c + 1) * P)
+                nc.tensor.matmul_mx(
+                    out=acc[j0, c][:], lhsT=sr_codes[:, rows].bitcast(FP8X4), lhsT_scale=sr_scales[:, rows],
+                    rhs=codes[:, cols].bitcast(FP8X4), rhs_scale=scales[:, cols], start=True, stop=False)
 
-        warm = psum.tile([P, HALF], F32, name="thr_ps")
-        nc.tensor.matmul_mx(
-            out=warm[:], lhsT=sr_mx[1][0][:].bitcast(FP8X4), lhsT_scale=sr_mx[1][1][:],
-            rhs=h_mx[1][0][:].bitcast(FP8X4), rhs_scale=h_mx[1][1][:], start=True, stop=True)
-
-        xw_got = [tile([P, HALF], U32, f"xw_got{a}") for a in range(2)]
-        for a in range(2):
-            nc.vector.tensor_copy(xw_got[a][:], xw_win[:].bitcast(U32).indirect(half_of(offs_t, a)))
-        w1_mx.append(quantise(w1_bf[1], P, "w11", "w11_codes"))
-        res = {(c, a): tile([P, HALF], F32, "w1_bf1" if (c, a) == (0, 1) else f"res{c}{a}") for c in range(M_TILES) for a in range(2)}
-        for c, j0, width in pieces:
-            cols = slice(j0 % HALF, j0 % HALF + width)
-            nc.tensor.matmul_mx(
-                out=acc[c, j0, width][:], lhsT=w1_mx[c][0][:].bitcast(FP8X4), lhsT_scale=w1_mx[c][1][:],
-                rhs=xw_got[j0 // HALF][:, cols].bitcast(FP8X4), rhs_scale=xs_plane[:, j0:j0 + width], start=False, stop=True)
-            dst = res[c, j0 // HALF]
-            if j0 % HALF:
-                nc.vector.tensor_scalar(dst[:, cols], acc[c, j0, width][:], thr_t[:, c, :], 0.0, ALU.add, ALU.max)
-            else:
-                nc.scalar.activation(dst[:, cols], acc[c, j0, width][:], ACT.Relu, bias=thr_t[:, c, :])
-            if cols.stop == HALF:
-                nc.sync.dma_start(out=out[c * P:(c + 1) * P, j0 + width - HALF:j0 + width], in_=dst[:])
+        xw_got = {j0: tile([P, width], U32, f"xw_got{j0}") for j0, width in stretches}
+        for j0, width in stretches:
+            nc.vector.tensor_copy(xw_got[j0][:], xw_win[:].bitcast(U32).indirect(entries(offs_t, j0, width)))
+        out_blocks = out.rearrange("(c p) j -> p c j", p=P)
+        for j0, width in stretches:
+            res = tile([P, M_TILES, width], F32, f"res{j0}")
+            for c in range(M_TILES):
+                rows = slice(c * P, (c + 1) * P)
+                nc.tensor.matmul_mx(
+                    out=acc[j0, c][:], lhsT=w1_codes[:, rows].bitcast(FP8X4), lhsT_scale=w1_scales[:, rows],
+                    rhs=xw_got[j0][:].bitcast(FP8X4), rhs_scale=xs_plane[:, j0:j0 + width], start=False, stop=True)
+                if j0 >= HALF and c == 1:
+                    nc.vector.tensor_scalar(res[:, c, :], acc[j0, c][:], thr_t[:, c, :], 0.0, ALU.add, ALU.max)
+                else:
+                    nc.scalar.activation(res[:, c, :], acc[j0, c][:], ACT.Relu, bias=thr_t[:, c, :])
+            nc.sync.dma_start(out=out_blocks[:, :, j0:j0 + width], in_=res[:])

@@ -21,7 +21,7 @@ PACK = 4
 HALF = S // 2
 M_TILES = N // P
 SCALE_ROWS = 16
-QUARTER = S // 4
+SCALAR_COLS = 5 * P // 8
 
 
 def tile_picked_ylista_nn_p_kernel(tc, x_words, x_scales, mem, w1, sr, thr, offs, slot, out):
@@ -58,19 +58,18 @@ def tile_picked_ylista_nn_p_kernel(tc, x_words, x_scales, mem, w1, sr, thr, offs
         thr_ps = psum.tile([P, P], F32, name="thr_ps")
         nc.tensor.transpose(thr_ps[:], thr_rows[:], ident[:])
 
-        def load_weights(weights, name):
-            raw = tile([P, PACK, N], F32, name)
-            nc.sync.dma_start(out=raw[:], in_=weights.rearrange("(p t) m -> p t m", t=PACK))
-            return raw
-
         nc.vector.tensor_copy(xs_got[:], xs_win[:].indirect(offs_t[:]))
-        sr_raw = load_weights(sr, "sr_raw")
-        w1_raw = load_weights(w1, "w1_raw")
+        sr_raw = tile([P, PACK, N], F32, "sr_raw")
+        w1_raw = [tile([P, PACK, P], F32, f"w1_raw{c}") for c in range(M_TILES)]
+        w1_rows = w1.rearrange("(p t) m -> p t m", t=PACK)
+        nc.sync.dma_start(out=sr_raw[:], in_=sr.rearrange("(p t) m -> p t m", t=PACK))
+        nc.sync.dma_start(out=w1_raw[0][:], in_=w1_rows[:, :, 0:P])
         xw_win = tile([P, T], I32, "xw_win")
         nc.sync.dma_start(out=xw_win[:], in_=x_words[0].rearrange("p n t -> p (n t)").bitcast(I32))
+        nc.sync.dma_start(out=w1_raw[1][:], in_=w1_rows[:, :, P:N])
         for q in range(4):
             first = P - SCALE_ROWS + 4 * q
-            queue = nc.gpsimd if q == 0 else nc.sync
+            queue = nc.gpsimd if q < 2 else nc.sync
             queue.dma_start(out=xs_plane[32 * q:32 * q + 4, :].bitcast(I32), in_=xs_got[first:first + 4, :].bitcast(I32))
 
         def entries(list_t, j0, width):
@@ -84,7 +83,7 @@ def tile_picked_ylista_nn_p_kernel(tc, x_words, x_scales, mem, w1, sr, thr, offs
             nc.scalar.activation(planes[:, t, :], window.indirect(entries(slot_t, HALF, HALF)), ACT.Copy)
 
         def interleave(grouped, raw):
-            return grouped[:].rearrange("p (c i) t -> p c t i", i=4), raw[:].rearrange("p t (c i) -> p c t i", i=4)
+            return grouped.rearrange("p (c i) t -> p c t i", i=4), raw.rearrange("p t (c i) -> p c t i", i=4)
 
         def quantise(grouped, width, name):
             codes = tile([P, width], U32, name + "_codes")
@@ -96,40 +95,44 @@ def tile_picked_ylista_nn_p_kernel(tc, x_words, x_scales, mem, w1, sr, thr, offs
         nc.vector.tensor_copy(
             h_bf[0][:].rearrange("p c t -> p (c t)").bitcast(I32).rearrange("p (c u) -> p c u", u=2),
             pairs[:].rearrange("p u c e -> p u (c e)").bitcast(I32).rearrange("p u c -> p c u"))
-        nc.vector.tensor_copy(*interleave(h_bf[1], planes))
-        sr_bf = tile([P, N, PACK], BF16, "sr_bf")
-        w1_bf = tile([P, N, PACK], BF16, "w1_bf")
-        nc.scalar.activation(*interleave(sr_bf, sr_raw), ACT.Copy)
+        nc.vector.tensor_copy(*interleave(h_bf[1][:], planes[:]))
+        sr_bf = [tile([P, P, PACK], BF16, f"sr_bf{c}") for c in range(M_TILES)]
+        for c in range(M_TILES):
+            nc.scalar.activation(*interleave(sr_bf[c][:], sr_raw[:, :, c * P:(c + 1) * P]), ACT.Copy)
+        w1_bf = [tile([P, P, PACK], BF16, f"w1_bf{c}") for c in range(M_TILES)]
         nc.scalar.activation(thr_t[:, :, 0], thr_ps[:, P - M_TILES:P], ACT.Copy)
-        nc.scalar.activation(*interleave(w1_bf, w1_raw), ACT.Copy)
-        h_mx = [quantise(h_bf[a], HALF, f"h{a}") for a in range(2)]
-        sr_codes, sr_scales = quantise(sr_bf, N, "sr")
-        w1_codes, w1_scales = quantise(w1_bf, N, "w1")
+        nc.scalar.activation(*interleave(w1_bf[0][:], w1_raw[0][:]), ACT.Copy)
+        nc.scalar.activation(*interleave(w1_bf[1][:, 0:SCALAR_COLS, :], w1_raw[1][:, :, 0:SCALAR_COLS]), ACT.Copy)
+        nc.gpsimd.tensor_scalar(*interleave(w1_bf[1][:, SCALAR_COLS:P, :], w1_raw[1][:, :, SCALAR_COLS:P]), 1.0, 0.0, ALU.mult, ALU.add)
+        h_mx, sr_mx = [], []
+        for i in range(2):
+            h_mx.append(quantise(h_bf[i], HALF, f"h{i}"))
+            sr_mx.append(quantise(sr_bf[i], P, f"sr{i}"))
+        w1_mx = [quantise(w1_bf[0], P, "w10")]
 
-        stretches = [(j0, QUARTER) for j0 in range(0, S, QUARTER)]
-        acc = {(j0, c): psum.tile([P, width], F32, name="thr_ps" if (j0, c) == (S - QUARTER, M_TILES - 1) else f"acc{j0}_{c}") for j0, width in stretches for c in range(M_TILES)}
-        for j0, width in stretches:
+        pieces = [(0, 0, HALF)] + [(0, j0, P) for j0 in range(HALF, S, P)] + [(1, j0, P) for j0 in range(0, S, P)]
+        acc = {piece: psum.tile([P, piece[2]], F32, name=f"acc{i}") for i, piece in enumerate(pieces)}
+        for c, j0, width in pieces:
             cols = slice(j0 % HALF, j0 % HALF + width)
             codes, scales = h_mx[j0 // HALF]
-            for c in range(M_TILES):
-                rows = slice(c * P, (c + 1) * P)
-                nc.tensor.matmul_mx(
-                    out=acc[j0, c][:], lhsT=sr_codes[:, rows].bitcast(FP8X4), lhsT_scale=sr_scales[:, rows],
-                    rhs=codes[:, cols].bitcast(FP8X4), rhs_scale=scales[:, cols], start=True, stop=False)
+            nc.tensor.matmul_mx(
+                out=acc[c, j0, width][:], lhsT=sr_mx[c][0][:].bitcast(FP8X4), lhsT_scale=sr_mx[c][1][:],
+                rhs=codes[:, cols].bitcast(FP8X4), rhs_scale=scales[:, cols], start=True, stop=False)
 
-        xw_got = {j0: tile([P, width], U32, f"xw_got{j0}") for j0, width in stretches}
-        for j0, width in stretches:
-            nc.vector.tensor_copy(xw_got[j0][:], xw_win[:].bitcast(U32).indirect(entries(offs_t, j0, width)))
-        out_blocks = out.rearrange("(c p) j -> p c j", p=P)
-        for j0, width in stretches:
-            res = tile([P, M_TILES, width], F32, f"res{j0}")
-            for c in range(M_TILES):
-                rows = slice(c * P, (c + 1) * P)
-                nc.tensor.matmul_mx(
-                    out=acc[j0, c][:], lhsT=w1_codes[:, rows].bitcast(FP8X4), lhsT_scale=w1_scales[:, rows],
-                    rhs=xw_got[j0][:].bitcast(FP8X4), rhs_scale=xs_plane[:, j0:j0 + width], start=False, stop=True)
-                if j0 >= HALF and c == 1:
-                    nc.vector.tensor_scalar(res[:, c, :], acc[j0, c][:], thr_t[:, c, :], 0.0, ALU.add, ALU.max)
-                else:
-                    nc.scalar.activation(res[:, c, :], acc[j0, c][:], ACT.Relu, bias=thr_t[:, c, :])
-            nc.sync.dma_start(out=out_blocks[:, :, j0:j0 + width], in_=res[:])
+        xw_got = [tile([P, HALF], U32, f"xw_got{a}") for a in range(2)]
+        for a in range(2):
+            nc.vector.tensor_copy(xw_got[a][:], xw_win[:].bitcast(U32).indirect(entries(offs_t, a * HALF, HALF)))
+        w1_mx.append(quantise(w1_bf[1], P, "w11"))
+        res = {(c, a): tile([P, HALF], F32, "w1_bf1" if (c, a) == (0, 1) else f"res{c}{a}") for c in range(M_TILES) for a in range(2)}
+        for c, j0, width in pieces:
+            cols = slice(j0 % HALF, j0 % HALF + width)
+            nc.tensor.matmul_mx(
+                out=acc[c, j0, width][:], lhsT=w1_mx[c][0][:].bitcast(FP8X4), lhsT_scale=w1_mx[c][1][:],
+                rhs=xw_got[j0 // HALF][:, cols].bitcast(FP8X4), rhs_scale=xs_plane[:, j0:j0 + width], start=False, stop=True)
+            dst = res[c, j0 // HALF]
+            if j0 % HALF:
+                nc.vector.tensor_scalar(dst[:, cols], acc[c, j0, width][:], thr_t[:, c, :], 0.0, ALU.add, ALU.max)
+            else:
+                nc.scalar.activation(dst[:, cols], acc[c, j0, width][:], ACT.Relu, bias=thr_t[:, c, :])
+            if cols.stop == HALF:
+                nc.sync.dma_start(out=out[c * P:(c + 1) * P, j0 + width - HALF:j0 + width], in_=dst[:])

from contextlib import ExitStack

import concourse.mybir as mybir
from concourse.masks import make_identity

K, T, S, H, N, U = 512, 2048, 512, 512, 256, 1024
FLOPS = 2 * (K + H) * N * S

F32 = mybir.dt.float32
BF16 = mybir.dt.bfloat16
I32 = mybir.dt.int32
U32 = mybir.dt.uint32
U16 = mybir.dt.uint16
U8 = mybir.dt.uint8
FP8X4 = mybir.dt.float8_e4m3fn_x4
ACT = mybir.ActivationFunctionType
ALU = mybir.AluOpType

P = 128
PACK = 4
HALF = S // 2
M_TILES = N // P
SCALE_ROWS = 16
SCALAR_COLS = 5 * P // 8


def tile_picked_ylista_nn_p_kernel(tc, x_words, x_scales, mem, w1, sr, thr, offs, slot, out):
    nc = tc.nc
    with ExitStack() as ctx:
        sb = ctx.enter_context(tc.tile_pool(name="sb", bufs=1))
        psum = ctx.enter_context(tc.psum_pool(name="psum", bufs=1))

        def tile(shape, dtype, name):
            return sb.tile(shape, dtype, name=name, align_bytes=256)

        slot_t = sb.tile([P, S // 16], U16, name="slot_t")
        offs_t = sb.tile([P, S // 16], U16, name="offs_t")
        xs_win = tile([P, T], U8, "xs_win")
        xs_got = tile([P, S], U8, "xs_got")
        xs_plane = tile([P, S], U8, "xs_plane")
        thr_rows = tile([P, P], F32, "thr_rows")
        nc.vector.memset(thr_rows[0:P - M_TILES, 0:P // 2], 0.0)
        nc.scalar.activation(thr_rows[0:P - M_TILES, P // 2:P], thr_rows[0:P - M_TILES, 0:P // 2], ACT.Copy)
        nc.vector.memset(xs_win[0:P - SCALE_ROWS, :].bitcast(I32), 0)
        nc.vector.memset(xs_plane[:].bitcast(I32), 0)

        nc.scalar.dma_start(out=xs_win[P - SCALE_ROWS:P, :].bitcast(I32), in_=x_scales[0].bitcast(I32))
        nc.sync.dma_start(offs_t[:], offs)
        mem_rows = mem.rearrange("(p t) u -> p t u", t=PACK)
        mem_t = [tile([P, 2, U], F32, f"mem{u}") for u in range(2)]
        nc.sync.dma_start(out=mem_t[0][:], in_=mem_rows[:, 0:2, :])
        nc.sync.dma_start(slot_t[:], slot)
        nc.sync.dma_start(out=mem_t[1][:], in_=mem_rows[:, 2:4, :])
        ident = tile([P, P], F32, "ident")
        thr_t = tile([P, M_TILES, 1], F32, "thr_t")
        nc.sync.dma_start(out=thr_rows[P - M_TILES:P, :], in_=thr.rearrange("(c p) o -> c (p o)", p=P))
        make_identity(nc, ident[:])
        thr_ps = psum.tile([P, P], F32, name="thr_ps")
        nc.tensor.transpose(thr_ps[:], thr_rows[:], ident[:])

        nc.vector.tensor_copy(xs_got[:], xs_win[:].indirect(offs_t[:]))
        sr_raw = tile([P, PACK, N], F32, "sr_raw")
        w1_raw = [tile([P, PACK, P], F32, f"w1_raw{c}") for c in range(M_TILES)]
        w1_rows = w1.rearrange("(p t) m -> p t m", t=PACK)
        nc.sync.dma_start(out=sr_raw[:], in_=sr.rearrange("(p t) m -> p t m", t=PACK))
        nc.sync.dma_start(out=w1_raw[0][:], in_=w1_rows[:, :, 0:P])
        xw_win = tile([P, T], I32, "xw_win")
        nc.sync.dma_start(out=xw_win[:], in_=x_words[0].rearrange("p n t -> p (n t)").bitcast(I32))
        nc.sync.dma_start(out=w1_raw[1][:], in_=w1_rows[:, :, P:N])
        for q in range(4):
            first = P - SCALE_ROWS + 4 * q
            queue = nc.gpsimd if q < 2 else nc.sync
            queue.dma_start(out=xs_plane[32 * q:32 * q + 4, :].bitcast(I32), in_=xs_got[first:first + 4, :].bitcast(I32))

        def entries(list_t, j0, width):
            return list_t[:, j0 // 16:(j0 + width) // 16]

        pairs = tile([P, 2, HALF, 2], BF16, "pairs")
        planes = tile([P, PACK, HALF], F32, "planes")
        for t in range(PACK):
            window = mem_t[t // 2][:, t % 2, :]
            nc.vector.tensor_copy(pairs[:, t // 2, :, t % 2], window.indirect(entries(slot_t, 0, HALF)))
            nc.scalar.activation(planes[:, t, :], window.indirect(entries(slot_t, HALF, HALF)), ACT.Copy)

        def interleave(grouped, raw):
            return grouped.rearrange("p (c i) t -> p c t i", i=4), raw.rearrange("p t (c i) -> p c t i", i=4)

        def quantise(grouped, width, name):
            codes = tile([P, width], U32, name + "_codes")
            scales = tile([P, width], U8, name + "_scales")
            nc.vector.quantize_mx(out=codes[:].bitcast(FP8X4), scales=scales[:], in_=grouped[:].rearrange("p c t -> p (c t)"))
            return codes, scales

        h_bf = [tile([P, HALF, PACK], BF16, f"h_bf{a}") for a in range(2)]
        nc.vector.tensor_copy(
            h_bf[0][:].rearrange("p c t -> p (c t)").bitcast(I32).rearrange("p (c u) -> p c u", u=2),
            pairs[:].rearrange("p u c e -> p u (c e)").bitcast(I32).rearrange("p u c -> p c u"))
        nc.vector.tensor_copy(*interleave(h_bf[1][:], planes[:]))
        sr_bf = [tile([P, P, PACK], BF16, f"sr_bf{c}") for c in range(M_TILES)]
        for c in range(M_TILES):
            nc.scalar.activation(*interleave(sr_bf[c][:], sr_raw[:, :, c * P:(c + 1) * P]), ACT.Copy)
        w1_bf = [tile([P, P, PACK], BF16, f"w1_bf{c}") for c in range(M_TILES)]
        nc.scalar.activation(thr_t[:, :, 0], thr_ps[:, P - M_TILES:P], ACT.Copy)
        nc.scalar.activation(*interleave(w1_bf[0][:], w1_raw[0][:]), ACT.Copy)
        nc.scalar.activation(*interleave(w1_bf[1][:, 0:SCALAR_COLS, :], w1_raw[1][:, :, 0:SCALAR_COLS]), ACT.Copy)
        nc.gpsimd.tensor_scalar(*interleave(w1_bf[1][:, SCALAR_COLS:P, :], w1_raw[1][:, :, SCALAR_COLS:P]), 1.0, 0.0, ALU.mult, ALU.add)
        h_mx, sr_mx = [], []
        for i in range(2):
            h_mx.append(quantise(h_bf[i], HALF, f"h{i}"))
            sr_mx.append(quantise(sr_bf[i], P, f"sr{i}"))
        w1_mx = [quantise(w1_bf[0], P, "w10")]

        pieces = [(0, 0, HALF)] + [(0, j0, P) for j0 in range(HALF, S, P)] + [(1, j0, P) for j0 in range(0, S, P)]
        acc = {piece: psum.tile([P, piece[2]], F32, name=f"acc{i}") for i, piece in enumerate(pieces)}
        for c, j0, width in pieces:
            cols = slice(j0 % HALF, j0 % HALF + width)
            codes, scales = h_mx[j0 // HALF]
            nc.tensor.matmul_mx(
                out=acc[c, j0, width][:], lhsT=sr_mx[c][0][:].bitcast(FP8X4), lhsT_scale=sr_mx[c][1][:],
                rhs=codes[:, cols].bitcast(FP8X4), rhs_scale=scales[:, cols], start=True, stop=False)

        xw_got = [tile([P, HALF], U32, f"xw_got{a}") for a in range(2)]
        for a in range(2):
            nc.vector.tensor_copy(xw_got[a][:], xw_win[:].bitcast(U32).indirect(entries(offs_t, a * HALF, HALF)))
        w1_mx.append(quantise(w1_bf[1], P, "w11"))
        res = {(c, a): tile([P, HALF], F32, "w1_bf1" if (c, a) == (0, 1) else f"res{c}{a}") for c in range(M_TILES) for a in range(2)}
        for c, j0, width in pieces:
            cols = slice(j0 % HALF, j0 % HALF + width)
            nc.tensor.matmul_mx(
                out=acc[c, j0, width][:], lhsT=w1_mx[c][0][:].bitcast(FP8X4), lhsT_scale=w1_mx[c][1][:],
                rhs=xw_got[j0 // HALF][:, cols].bitcast(FP8X4), rhs_scale=xs_plane[:, j0:j0 + width], start=False, stop=True)
            dst = res[c, j0 // HALF]
            if j0 % HALF:
                nc.vector.tensor_scalar(dst[:, cols], acc[c, j0, width][:], thr_t[:, c, :], 0.0, ALU.add, ALU.max)
            else:
                nc.scalar.activation(dst[:, cols], acc[c, j0, width][:], ACT.Relu, bias=thr_t[:, c, :])
            if cols.stop == HALF:
                nc.sync.dma_start(out=out[c * P:(c + 1) * P, j0 + width - HALF:j0 + width], in_=dst[:])
